import numpy as np, ml_dtypes
CORES = [24,25,26,27,28,29,30,31]
N = 8
BF = ml_dtypes.bfloat16
def gentries(a):
    return np.ascontiguousarray(a.reshape(8, 16, -1).transpose(0, 2, 1)).reshape(8, -1)
def gtable(e):
    e = np.asarray(e); return np.ascontiguousarray(e.reshape(8, -1, 16).transpose(0, 2, 1)).reshape(128, -1).astype(np.int32)
C, L, HOPS = 512, 8, (1, 2, 3, 4, 5, 6)
W = C * L; RO = len(HOPS); B = 2 ** RO; NB = C // B
def lay(rng):
    P = np.argsort(rng.random((8, W)), axis=-1)
    for g in range(8):
        for k, v in ((W - 1, W - 1), (W - 2, 0)):
            j = int(np.flatnonzero(P[g] == v)[0]); P[g, j] = P[g, k]; P[g, k] = v
    return P.reshape(8, NB, B, L)
def turned(rng, P):
    ix = (np.arange(L) + rng.integers(0, L, (N, NB, B))[..., None]) % L
    return np.array(np.take_along_axis(np.broadcast_to(P, (N,) + P.shape), np.broadcast_to(ix[:, None], (N,) + P.shape), -1))
def mix(rng, e, b):
    for q in range(N):
        for g in range(8): e[q, g, b] = rng.permutation(e[q, g, b].reshape(-1)).reshape(B, L)
def pack(e, x):
    return {"o": np.stack([gtable(a) for a in e.reshape(N, 8, W)]), "x": np.ascontiguousarray(x.reshape(N, 128, W)).astype(np.float32).astype(BF)}
def place(P, v):
    inv = np.argsort(P.reshape(8, W), axis=-1)
    return np.take_along_axis(v.reshape(N, 8, 16, W), np.broadcast_to(inv[None, :, None, :], (N, 8, 16, W)), -1)
def parity():
    return np.array([bin(i).count("1") % 2 for i in range(B)])
def setup_inputs(rng):
    return pack(np.argsort(rng.random((N, 8, W)), axis=-1), rng.integers(0, 16, (N, 8, 16, W)))
def setup_inputs_spread(rng):
    hi = rng.integers(1, 17, (N, 8, 1, W)) * (rng.random((N, 8, 1, W)) > 0.0625)
    v = np.floor(hi * rng.random((N, 8, 16, W)) ** rng.choice(np.array([0.5, 1.0, 2.0, 4.0]), (N, 8, 16, 1)))
    return pack(np.argsort(rng.random((N, 8, W)), axis=-1), v)
def setup_inputs_ends(rng):
    P = lay(rng); e = turned(rng, P); v = 15 * rng.integers(0, 2, (N, 8, 16, NB, B, L)); flip = rng.integers(0, 2, (N, 1, 1, 1, 1)); par = parity()[:, None]
    for b in range(NB):
        k = (NB - 1 - b) % 4
        if k == 2: mix(rng, e, b); continue
        v[:, :, :, b] = 15 * ((par if k != 1 else 0 * par) ^ flip)
        if k < 2: v[:, 7, 15, b] = np.where(rng.random((N, B, L)) < 0.5, 15 - v[:, 7, 15, b], v[:, 7, 15, b])
    return pack(e, place(P, v))
def setup_inputs_edge(rng):
    P = lay(rng); e = turned(rng, P); v = rng.integers(0, 2, (N, 8, 16, NB, B, L)); flip = rng.integers(0, 2, (N, 1, 1, 1, 1)); par = parity()[:, None]
    for b in range(NB):
        k = (NB - 1 - b) % 4
        if k == 0:
            v[:, :, :, b] = 15 * (par ^ flip); v[:, 7, 15, b] = rng.integers(7, 10, (N, B, L))
        if k == 1:
            h = rng.integers(0, 15, (N, 8, 16, 1, L // 2)); v[:, :, :, b] = h[..., np.arange(L) % (L // 2)]
            v[:, 0, 0, b, :, 0] += rng.integers(0, 2, (N, B))
        if k == 2: mix(rng, e, b)
        if k == 3: v[:, :, :, b] = rng.integers(0, 16, (N, 8, 16, B, 1))
    return pack(e, place(P, v))
def setup_inputs_gap(rng):
    P = lay(rng); e = turned(rng, P); v = np.zeros((N, 8, 16, NB, B, L), np.int64); flip = rng.integers(0, 2, (N, 1, 1, 1, 1)); par = parity()[:, None]
    col = np.arange(L)[None, :]; z = int(rng.integers(0, 4))
    for b in range(NB):
        k = (NB - 1 - b) % 4
        if k == 0 or k == 3:
            v[:, :, :, b] = 15 * ((col % 2 if k == 0 else col // (L // 2)) ^ flip)
            v[:, 7, 15, b] = np.abs(v[:, 7, 15, b] - rng.integers(0, 2, (N, B, L)))
        if k == 1:
            for q in range(N):
                fl = int(flip[q, 0, 0, 0, 0]); u = 15 * ((col % 2) ^ (0 * par) ^ fl); w = 15 * ((col % 2) ^ par ^ fl)
                for m in range(8):
                    g = (m + 2 * (q + z)) % 8
                    if m < 3: v[q, g, :, b] = w
                    if m == 3 or m == 6: v[q, g, :, b] = u
                    if m == 4 or m == 5:
                        for i in rng.permutation(16)[:8]: v[q, g, int(i), b] = u
                    if m == 7: v[q, g, :, b] = rng.integers(0, 16, (16, B, 1))
        if k == 2:
            v[:, :, :, b] = 15 * (par ^ flip)
            up = par ^ flip[:, 0, 0]; h = rng.integers(1, 16, (N, 1, 1))
            v[:, 7, 15, b] = np.where(np.arange(L) == rng.integers(0, L, (N, B, 1)), h - up, 15 * up)
    return pack(e, place(P, v))
def setup_inputs_corners(rng):
    one = np.arange(W); e = np.argsort(rng.random((N, 8, W)), axis=-1)
    for g in range(8):
        both = rng.permutation(W)
        for q in range(N):
            h = (g + 2 * (q % 2)) % 8
            if h == 0: e[q, g] = one
            if h == 1: e[q, g] = one[::-1]
            if h == 2: e[q, g] = np.roll(one, 1)
            if h == 3: e[q, g] = both
            if h == 4: e[q, g] = one.reshape(L, C).T.reshape(-1)
            if h == 5: e[q, g] = np.argsort(both)
            if h == 6: e[q, g] = np.roll(one.reshape(C, L), q + 1, axis=1).reshape(-1)
    x = rng.integers(0, 16, (N, 8, 16, W)); w = rng.permutation(N)
    x[w[0]] = 15; x[w[1], :7] = 0; x[w[2], ::2] = 15 * rng.integers(0, 2, (4, 16, W))
    return pack(e, x)
def check_inputs(d):
    bad = []; v = np.asarray(d["x"]).astype(np.float32); c = np.asarray(d["o"])
    if not np.all((v >= 0) & (v <= 15)): bad.append("range of x")
    if not np.all(v == np.floor(v)): bad.append("whole numbers of x")
    if np.min(c) < 0 or np.max(c) > W - 1: bad.append("range of o")
    if np.any(np.sort(np.stack([gentries(a) for a in c]), axis=-1) != np.arange(W)): bad.append("permutation of o")
    return bad
def reference(o, x):
    cy = np.stack([gentries(a) for a in o]).astype(np.int64)
    xv = x.astype(np.float32).astype(np.int32).reshape(N, 8, 16, W); num = np.arange(C)
    for t in range(RO):
        lo = num[(num >> t) % 2 == 0]; hi = lo + 2 ** t; roots = []
        for q in range(N):
            cq = cy[q].reshape(8, C, L); a = cq[:, lo]; b = cq[:, hi]
            xa = np.take_along_axis(xv[q], a.reshape(8, 1, -1), 2).reshape(128, C // 2, L)
            xb = np.take_along_axis(xv[q], b.reshape(8, 1, -1), 2).reshape(128, C // 2, L)
            score = np.stack([np.add.reduce(np.abs(xa - np.roll(xb, -k, axis=2)), axis=(0, 2)) for k in range(L)])
            s = np.argmin(score, axis=0)
            ix = np.broadcast_to((np.arange(L)[None, :] + s[:, None]) % L, b.shape)
            bs = np.take_along_axis(b, ix, 2)
            f = np.zeros((8, W), np.int64)
            np.put_along_axis(f, a.reshape(8, -1), bs.reshape(8, -1), 1)
            np.put_along_axis(f, bs.reshape(8, -1), np.roll(a, -1, axis=2).reshape(8, -1), 1)
            roots.append(f)
        cy = np.stack([np.take_along_axis(roots[(r - HOPS[t]) % N], cy[r], 1) for r in range(N)])
    return {"yo": np.stack([gtable(e) for e in cy]).astype(np.float32)}

@@ -1,0 +1,550 @@
+from concourse.mybir import AluOpType, AxisListType, ActivationFunctionType
+
+RO = 6
+HOPS = (1, 2, 3, 4, 5, 6)
+N = 8
+
+SCRATCH = {
+    "xs": ("sbuf", [128, 4096], "bfloat16"),
+    "xo": ("sbuf", [128, 4096], "bfloat16"),
+    "xt": ("sbuf", [128, 4096], "bfloat16"),
+    "tab": ("sbuf", [128, 4096], "bfloat16"),
+    "ft": ("sbuf", [128, 4096], "bfloat16"),
+    "fo": ("sbuf", [128, 4096], "bfloat16"),
+    "inv0": ("sbuf", [128, 4096], "bfloat16"),
+    "inv1": ("sbuf", [128, 4096], "bfloat16"),
+    "junk": ("sbuf", [128, 4096], "bfloat16"),
+    "oi": ("sbuf", [128, 256], "int32"),
+    "lo": ("sbuf", [128, RO * 256], "uint16"),
+    "lr": ("sbuf", [128, RO * 256], "uint16"),
+    "lf": ("sbuf", [128, RO * 256], "uint16"),
+    "sa": ("sbuf", [128, RO * 256], "uint16"),
+    "sf": ("sbuf", [128, RO * 256], "uint16"),
+    "li": ("sbuf", [128, 256], "uint16"),
+    "ow": ("sbuf", [128, RO * 512], "bfloat16"),
+    "so": ("sbuf", [128, RO * 512], "bfloat16"),
+    "bo": ("sbuf", [128, 1024], "bfloat16"),
+    "ys": ("sbuf", [128, 256], "float32"),
+    "yl": ("sbuf", [128, 256], "float32"),
+    "dm": ("sbuf", [128, 4 * 512], "bfloat16"),
+    "pm": ("sbuf", [128, 3 * 128], "bfloat16"),
+    "idn": ("sbuf", [128, 128], "bfloat16"),
+    "zo": ("sbuf", [128, 144], "bfloat16"),
+    "zi": ("sbuf", [128, 144], "bfloat16"),
+    "rm": ("sbuf", [128, 64], "float32"),
+    "lht": ("sbuf", [128, 256], "bfloat16"),
+    "lh": ("sbuf", [128, 256], "float32"),
+    "mk": ("sbuf", [128, RO * 64], "float32"),
+    "cj": ("sbuf", [128, RO * 64], "float32"),
+    "bs": ("sbuf", [128, RO * 64], "float32"),
+    "one": ("sbuf", [128, 32], "bfloat16"),
+    "srow": ("sbuf", [128, 16], "bfloat16"),
+    "pi": ("sbuf", [128, 4], "int32"),
+    "pf": ("sbuf", [128, 4], "float32"),
+    "hl": ("sbuf", [128, 512], "bfloat16"),
+    "ramp": ("sbuf", [128, 64], "float32"),
+    "hc": ("sbuf", [128, 64], "float32"),
+    "sc": ("sbuf", [128, 32], "float32"),
+    "km": ("sbuf", [128, 4], "float32"),
+    "rh": ("sbuf", [128, 128], "float32"),
+    "i1": ("sbuf", [128, 64], "int32"),
+    "i2": ("sbuf", [128, 64], "int32"),
+    "i3": ("sbuf", [128, 64], "float32"),
+    "rl": ("sbuf", [128, 64], "uint16"),
+    "d0": ("psum", [128, 512], "float32"),
+    "d1": ("psum", [128, 512], "float32"),
+    "d2": ("psum", [128, 512], "float32"),
+    "d3": ("psum", [128, 512], "float32"),
+    "t0": ("psum", [128, 1024], "bfloat16"),
+    "t1": ("psum", [128, 1024], "bfloat16"),
+    "pw": ("psum", [128, 512], "float32"),
+    "pk": ("psum", [128, 512], "float32"),
+}
+SEMAPHORES = (["cV", "cS", "cP", "cG", "ldo", "ldx", "iot", "tabd", "owd", "sent", "st"]
+              + ["%s%d" % (n, t) for n in ("aa", "ab", "ac", "ar", "af", "ao") for t in range(RO + 1)])
+PSUM = ("d0", "d1", "d2", "d3", "t0", "t1", "pw", "pk")
+
+V_SEQ = "ga0 ga1 e0 i01 r0 ga2 e1 r0 r0 r1 e2 r1 r1 ga3 r1 r2 e3 r2 r2 r2 r3 r3 r3".split()
+S_SEQ = "gb0 gb1 i12 r0 r0 gb2 r0 r0 r0 r1 r1 r1 r1 gb3 r2 r2 r2 r2 r3 r3 r3 r3 r3".split()
+V_SEQ0 = "s0 s1 u0 s2 s3 e0 s4 r0 e1 e2 r0 s5 r0 e3 r2 s6 r2 r2 r2 s7 r2 r2 r3 r3 r3".split()
+S_SEQ0 = "ga0 gb0 c0 gb1 ga1 ga2 r0 gb2 gb3 r0 r0 ga3 r0 r0 r1 r1 r1 c3 r1 r1 r1 r1 r1 r2 r2 r3 r3 r3 r3 r3".split()
+COST = {"g": 0.9, "e": 0.6, "r": 0.62, "s": 2.05, "u": 1.0, "c": 0.6, "i": 0.9}
+
+
+TABK = ["tab", "tab1", "tab2", "tab3"]
+BIG64 = 1.5 * 2.0 ** 29
+CUTS = (0, 1, 2, 4)
+LAST_CUTS = (0, 3, 4)
+SHARE = (32, 32, 26, 26)
+LAST_SHARE = (32, 32, 32, 32)
+
+
+def chunk(cuts, q):
+    return max(k for k in range(len(cuts) - 1) if cuts[k] <= q)
+
+
+def pieces(weights):
+    dims = []
+    for w in weights:
+        if dims and w == dims[-1][0] * dims[-1][1]:
+            dims[-1][1] *= 2
+        else:
+            dims.append([w, 2])
+    low = dims[:3]
+    n = 1
+    for d in low:
+        n *= d[1]
+    nb = n.bit_length() - 1
+    out = []
+    for h in range(2 ** (len(weights) - nb)):
+        off = sum(weights[nb + b] for b in range(len(weights) - nb) if h >> b & 1)
+        out.append((h * n, n, off, [list(d) for d in reversed(low)]))
+    return out
+
+
+CODE_W = ([0, 4, 8, 1, 2], [0, 4, 8, 1, 2], [4, 0, 8, 1, 2], [4, 8, 0, 1, 2], [4, 8, 1, 0, 2], [4, 8, 1, 2, 0])
+
+
+def rank_program(g, core, T, topo):
+    rank = T.rank_of(core)
+    if rank is None:
+        return
+    A = AluOpType
+    AF = ActivationFunctionType
+    Q = {"V": g.vector, "S": g.scalar, "P": g.tensor, "G": g, "Y": g.sync}
+    count = {}
+    known = {e: {} for e in Q}
+    lastw = {}
+    readers = {}
+
+    def wait(e, tok):
+        if tok is None or (e == "P" and tok[0] == "cP"):
+            return
+        if known[e].get(tok[0], 0) < tok[1]:
+            Q[e].wait_ge(T.sem[tok[0]], tok[1])
+            known[e][tok[0]] = tok[1]
+
+    def deps(e, rd, wr):
+        toks = []
+        for k in rd:
+            toks.append(lastw.get(k))
+            if k in PSUM:
+                toks += [t for t in readers.get(k, []) if t[0] != "c" + e]
+        for k in wr:
+            toks.append(lastw.get(k))
+            toks += readers.get(k, [])
+        best = {}
+        for t in toks:
+            if t is not None and best.get(t[0], 0) < t[1]:
+                best[t[0]] = t[1]
+        for s in best:
+            wait(e, (s, best[s]))
+
+    def mark(tok, rd, wr):
+        for k in rd:
+            readers.setdefault(k, []).append(tok)
+        for k in wr:
+            lastw[k] = tok
+            readers[k] = []
+
+    def op(e, fn, rd=(), wr=()):
+        deps(e, rd, wr)
+        s = "c" + e
+        count[s] = count.get(s, 0) + 1
+        fn().then_inc(T.sem[s], 1)
+        mark((s, count[s]), rd, wr)
+
+    def dmas(sem, items):
+        for e, out, in_, rd, wr in items:
+            deps(e, rd, wr)
+            Q[e].dma_start(out, in_).then_inc(T.sem[sem], 16)
+            count[sem] = count.get(sem, 0) + 16
+        for e, out, in_, rd, wr in items:
+            mark((sem, count[sem]), rd, wr)
+
+    def arrives(key, sem, n):
+        count[sem] = n
+        lastw[key] = (sem, n)
+
+    def peer(d):
+        return T.cores[(rank + d) % N]
+
+    def width(dst):
+        return len(topo.engines(core, dst))
+
+    def send(d, out, in_, sem, rd):
+        dst = peer(d)
+        deps("G", rd, ())
+        rid, pid, _ = topo.addr(dst)
+        g.remote_dma(out, in_, T.sem[sem], T.sem.sent, pid, rid, topo.mask(core, dst))
+        count["sent"] = count.get("sent", 0) + width(dst)
+
+    def from_(d):
+        return len(topo.engines(peer(-d), core))
+
+    def gather(e, out, win, off, rd, wr):
+        if e == "V":
+            op(e, lambda: g.vector.tensor_copy(out, win.indirect(off)), rd, wr)
+        else:
+            op(e, lambda: g.scalar.activation(out, win.indirect(off), AF.Copy), rd, wr)
+
+    def mm(out, lhsT, rhs, start, stop, rd, wr):
+        op("P", lambda: g.tensor.matmul(out, lhsT, rhs, start, stop), rd, wr)
+
+    def sel(ap, pat, cmp, fill, base, cm, key):
+        op("G", lambda: g.affine_select(ap, ap, pat, cmp, fill, base, cm), [key], [key])
+
+    def iota(ap, pat, base, cm, key, small=True):
+        if small:
+            op("G", lambda: g.iota(ap, pat, base, cm, allow_small_or_imprecise_dtypes=True), [], [key])
+        else:
+            op("G", lambda: g.iota(ap, pat, base, cm), [], [key])
+
+    def memset(ap, v, key):
+        op("V", lambda: g.vector.memset(ap, v), [], [key])
+
+    def vcopy(out, in_, rd, wr):
+        op("V", lambda: g.vector.tensor_copy(out, in_), rd, wr)
+
+    def wrap(bank, col, src, skeys, z, c0, n, r0=0, r1=16):
+        for r in range(r0, r1):
+            mm(T[bank][:, col:col + n], T[z][:, 15 - r:143 - r], src[:, 16 * c0 + r:16 * (c0 + n):16],
+               r == 0, r == 15, skeys + [z], [bank])
+
+    def quarters(name):
+        return ["%s%d%s" % (name, q, h) for q in range(4) for h in "ab"]
+
+    arrives("lr0", "ar0", from_(-1))
+    for t in range(1, RO + 1):
+        h = HOPS[t - 1]
+        arrives("loa%d" % t, "aa%d" % t, from_(h))
+        arrives("lob%d" % t, "ab%d" % t, from_(h))
+        if t < RO:
+            arrives("loc%d" % t, "ac%d" % t, from_(h))
+            arrives("lr%d" % t, "ar%d" % t, from_(h - HOPS[t]))
+            arrives("lf%d" % t, "af%d" % t, from_(h))
+            arrives("ow%d" % t, "ao%d" % t, from_(h))
+
+    dmas("ldo", [("Y", T.oi[:], T.o[:], [], ["oi"])])
+    dmas("ldx", [("S", T.xs[:], T.x[:], [], ["xs"])])
+    iota(T.pi[:, 0:1], [[0, 1]], 0, 1, "pi", False)
+    iota(T.ramp[:], [[1, 64]], 0, 0, "ramp")
+    memset(T.idn[:], 0.0, "idn")
+    memset(T.dm[:, 1536:2048], 0.0, "dm3")
+    op("V", lambda: g.vector.tensor_scalar(T.pi[:, 1:2], T.pi[:, 0:1], 8, None, A.bitwise_and), ["pi"], ["pi8"])
+    memset(T.pm[:], 0.0, "pm")
+    vcopy(T.pf[:, 1:2], T.pi[:, 1:2], ["pi8"], ["pf1"])
+    memset(T.zo[:], 0.0, "zo")
+    op("V", lambda: g.vector.tensor_scalar(T.pf[:, 0:1], T.pf[:, 1:2], -1.0, 8.0, A.mult, A.add), ["pf1"], ["pf0"])
+    op("V", lambda: g.vector.tensor_scalar(T.tab[:, 0:64], T.ramp[:], T.pf[:, 1:2], 0.125, A.mult, A.mult), ["ramp", "pf1"], ["tab"])
+    op("V", lambda: g.vector.tensor_scalar(T.hc[:], T.ramp[:], T.pf[:, 0:1], 8.0, A.mult, A.mult), ["ramp", "pf0"], ["hc"])
+    for k in range(3):
+        n = 64 << k
+        op("V", lambda: g.vector.tensor_scalar(T.tab[:, n:2 * n], T.tab[:, 0:n], T.hc[:, n // 64:n // 64 + 1], None, A.add),
+           ["tab", "hc"], ["tab"])
+    for k in range(3):
+        n = 512 << k
+        op("S", lambda: g.scalar.activation(T.tab[:, n:2 * n], T.tab[:, 0:n], AF.Identity, bias=T.hc[:, n // 64:n // 64 + 1]),
+           ["tab", "hc"] + TABK[1:k + 1], [TABK[k + 1]])
+    vcopy(T.lo[:, 0:256], T.oi[:], ["oi"], ["loa0", "lob0", "loc0"])
+    sel(T.idn[:], [[-1, 128]], A.not_equal, 1.0, 0, 1, "idn")
+    d3 = T.dm[64:128, 1536:2048]
+    deps("G", ["idn"], [])
+    sel(d3, [[-1, 8], [-1, 8], [-8, 8]], A.not_equal, -1.0, 0, 1, "dm3")
+    sel(d3, [[-1, 8], [-1, 8], [-8, 8]], A.not_equal, -1.0, 8, 1, "dm3")
+    sel(d3, [[0, 64], [-8, 8]], A.is_ge, 0.0, 0, 1, "dm3")
+    sel(d3, [[0, 64], [8, 8]], A.is_ge, 0.0, 7, -1, "dm3")
+    sel(T.dm[0:64, 1536:2048], [[-1, 8], [0, 8], [-8, 8]], A.not_equal, 1.0, 0, 1, "dm3")
+
+    def perm(t):
+        sel(T.pm[:, 128 * t:128 * t + 128], [[-8 * 2 ** t, 8 // 2 ** t], [-64, 2], [-1, 8 * 2 ** t]],
+            A.not_equal, 1.0, 0, 1, "pm")
+
+    def round_consts(t):
+        c = 64 * t
+        side = [0] * 6
+        if t > 0:
+            side[t - 1] = 1
+        u = 32 if t == 0 else 1
+        for a, n, off, pat in pieces([-2 * s for s in side]):
+            iota(T.mk[:, c + a:c + a + n], pat, u + off, 0, "mk%d" % t)
+        for a, n, off, pat in pieces([-8 * w for w in CODE_W[t]] + [0]):
+            sel(T.mk[:, c + a:c + a + n], pat, A.is_ge, 0.0, off, 1, "mk%d" % t)
+        for a, n, off, pat in pieces([8 * w for w in CODE_W[t]] + [0]):
+            sel(T.mk[:, c + a:c + a + n], pat, A.is_ge, 0.0, 7 + off, -1, "mk%d" % t)
+        for a, n, off, pat in pieces(side[:5] + [-u]):
+            iota(T.cj[:, c + a:c + a + n], pat, off, u, "cj%d" % t)
+        w = [((16 if t else 1) << b) * (1 - 2 * side[b]) for b in range(5)] + [0]
+        for a, n, off, pat in pieces(w):
+            iota(T.bs[:, c + a:c + a + n], pat, off + sum((16 << b) * side[b] for b in range(5)), 0, "bs%d" % t)
+
+    perm(0)
+    mm(T.pw[:, 0:512], T.pm[:, 0:128], T.dm[:, 1536:2048], True, True, ["pm", "dm3"], ["pw"])
+    send(-1, T.lr[:, 0:256], T.lo[:, 0:256], "ar0", ["loa0"])
+    for name, n, v in (("zi", 144, 0), ("rm", 64, 0), ("lht", 256, 1), ("one", 32, 1)):
+        iota(T[name][:], [[0, n]], v, 0, name)
+    for z, o in (("zo", 0), ("zi", 4)):
+        sel(T[z][:, 15:128:16], [[16, 8]], A.not_equal, 1.0, o, -1, z)
+        sel(T[z][:, 15:128:16], [[16, 8]], A.not_equal, 1.0, o + 8, -1, z)
+    perm(1)
+    perm(2)
+    for q0 in range(2):
+        sel(T.lht[:, 128 * q0:128 * q0 + 128], [[0, 16], [-16, 8]], A.is_ge, 0.0, -8 * q0, 1, "lht")
+        sel(T.lht[:, 128 * q0:128 * q0 + 128], [[0, 16], [16, 8]], A.is_ge, 0.0, 8 * q0 + 7, -1, "lht")
+    sel(T.rm[:], [[-1, 8], [-8, 8]], A.not_equal, 8.0, 0, 1, "rm")
+    sel(T.rm[:], [[-1, 8], [-8, 8]], A.not_equal, 8.0, -64, 1, "rm")
+    iota(T.srow[:], [[0, 2], [1, 8]], 0, 0, "srow")
+    round_consts(0)
+
+    def copy(e, out, in_, rd, wr):
+        if e == "V":
+            vcopy(out, in_, rd, wr)
+        else:
+            op(e, lambda: g.scalar.activation(out, in_, AF.Copy), rd, wr)
+
+    def late_const(e, k):
+        if k == 0:
+            copy(e, T.dm[:, 0:512], T.pw[:, 0:512], ["pw"], ["dm0"])
+        elif k < 3:
+            bank = "d%d" % (k + 1)
+            mm(T[bank][:, 0:512], T.pm[:, 128 * k:128 * k + 128], T.dm[:, 1536:2048], True, True, ["pm", "dm3"], [bank])
+            copy(e, T.dm[:, 512 * k:512 * k + 512], T[bank][:, 0:512], [bank], ["dm%d" % k])
+        else:
+            for q0 in range(2):
+                mm(T.pw[:, 128 * q0:128 * q0 + 128], T.lht[:, 128 * q0:128 * q0 + 128], T.idn[:], True, True,
+                   ["lht", "idn"], ["pw"])
+            copy(e, T.lh[:], T.pw[:, 0:256], ["pw"], ["lh"])
+
+    def window_dmas(dst, col, key, gs):
+        dmas("owd", [("Y", dst[16 * y:16 * y + 16, col:col + 512], T.fo[0:128:8, 512 * y:512 * y + 512],
+                      ["fo%da" % (y // 2), "fo%db" % (y // 2)], [key]) for y in gs])
+
+    def scores(t):
+        vs, ss = (V_SEQ0, S_SEQ0) if t == 0 else (V_SEQ, S_SEQ)
+        c0 = 256 * t
+        dk = min(t, 3)
+        steps = []
+        ready = {}
+        clock = {"V": 0.0, "S": 0.0}
+        pos = {"V": 0, "S": 0}
+        seq = {"V": vs, "S": ss}
+        used = [0] * 4
+        nb = {"V": 0, "S": 0}
+        free = {}
+        while pos["V"] < len(vs) or pos["S"] < len(ss):
+            cand = []
+            for e in "VS":
+                if pos[e] < len(seq[e]):
+                    s = seq[e][pos[e]]
+                    q = s[-1]
+                    need = {"e": ["ga" + q, "gb" + q], "r": ["e" + q] + (["c0"] if t == 0 else [])}.get(s[0], [])
+                    if all(k in ready for k in need):
+                        cand.append((max([clock[e]] + [ready[k] + 0.6 for k in need]), e, s, need))
+            at, e, s, need = min(cand)
+            if s[0] == "e":
+                tt = max([ready[k] for k in need] + [ready.get("e%d" % (int(s[1]) - 2), 0.0)])
+                steps.append((tt, 0, "P", "t", int(s[1]), None))
+                at = max(at, tt)
+                steps.append((at, 1, e, s, None, None))
+            elif s[0] == "r":
+                n = 8 * int(s[1]) + used[int(s[1])]
+                used[int(s[1])] += 1
+                bank = "d%d" % ((0 if e == "V" else 2) + nb[e] % 2)
+                nb[e] += 1
+                steps.append((max([free.get(bank, 0.0)] + [ready[k] for k in need]), 0, "P", "d", n, bank))
+                steps.append((at, 1, e, "r", n, bank))
+                free[bank] = at + COST["r"]
+            else:
+                steps.append((at, 1, e, s, None, None))
+            clock[e] = at + COST[s[0]] * (int(s[2]) - int(s[1]) if s[0] == "i" else 1)
+            ready[s] = clock[e]
+            pos[e] += 1
+        assert used == [8] * 4
+        order = sorted(range(len(steps)), key=lambda i: (steps[i][0] - (0.0 if steps[i][1] else 1e-6 * 0), i))
+        for i in order:
+            at, _, e, s, n, bank = steps[i]
+            if s[0] == "g":
+                q, hf = int(s[2]), "ab".index(s[1])
+                a = 64 * q + 32 * hf
+                gather(e, T.xo[:, 16 * a:16 * a + 512], T.xs[:, 0:4096], T.lo[:, c0 + a:c0 + a + 32],
+                       ["xs", "lo%s%d" % ("abc"[chunk(CUTS, q)], t)], ["xo%d%s" % (q, s[1])])
+            elif s == "t":
+                tb = "t%d" % (n % 2)
+                for b in range(8):
+                    y, b2 = 2 * n + b // 4, b % 4
+                    rd = ["xo%d%s" % (n, "ab"[b // 4]), "idn"]
+                    if t <= 3:
+                        parts = [(0, 128, 512 * y + 128 * b2)]
+                    elif t == 4:
+                        a = 512 * y + 256 * (b2 >> 1) + 64 * (b2 & 1)
+                        parts = [(0, 64, a), (64, 64, a + 128)]
+                    else:
+                        a = 512 * y + 64 * b2
+                        parts = [(0, 64, a), (64, 64, a + 256)]
+                    for p, m, a in parts:
+                        op("P", lambda: g.tensor.transpose(T[tb][p:p + m, 128 * b:128 * b + 128], T.xo[:, a:a + m], T.idn[:]),
+                           rd, [tb])
+            elif s[0] == "e":
+                q = int(s[1])
+                vcopy(T.xt[:, 1024 * q:1024 * q + 1024], T["t%d" % (q % 2)][:, 0:1024], ["t%d" % (q % 2)], ["xt%d" % q])
+            elif s == "d":
+                for ml in range(4):
+                    a = 512 * dk + 128 * ml
+                    mm(T[bank][:, 128 * ml:128 * ml + 128], T.dm[:, a:a + 128], T.xt[:, 128 * n:128 * n + 128], True, True,
+                       ["dm%d" % dk, "xt%d" % (n // 8)], [bank])
+            elif s == "r":
+                col = 8 * (n % 4) + n // 4
+                if e == "V":
+                    op(e, lambda: g.vector.tensor_reduce(T.sc[:, col:col + 1], T[bank][:, 0:512], AxisListType.X, A.add,
+                                                         apply_absolute_value=True), [bank], ["sc%d" % col])
+                else:
+                    j = 512 * (n % 8)
+                    op(e, lambda: g.scalar.activation(T.junk[:, j:j + 512], T[bank][:, 0:512], AF.Abs,
+                                                      accum_out=T.sc[:, col:col + 1]), [bank], ["sc%d" % col, "junk%d" % (n % 8)])
+            elif s[0] == "s":
+                q = int(s[1])
+                op(e, lambda: g.vector.tensor_copy(T.inv0[:, 0:4096].indirect(T.lo[:, 32 * q:32 * q + 32]),
+                                                   T.tab[:, 512 * q:512 * q + 512]),
+                   [TABK[q.bit_length()], "lob0"], quarters("inv0"))
+            elif s[0] == "u":
+                op(e, lambda: g.vector.tensor_scalar(T.hl[:, 0:256], T.oi[:], BIG64, -BIG64, A.add, A.add), ["oi"], ["hl0"])
+                op(e, lambda: g.vector.tensor_tensor(T.hl[:, 256:512], T.oi[:], T.hl[:, 0:256], A.subtract), ["oi", "hl0"], ["hl1"])
+                op(e, lambda: g.vector.tensor_scalar(T.pf[:, 2:3], T.pf[:, 0:1], 32.0, None, A.mult), ["pf0"], ["pf2"])
+                dmas("owd", [("Y", T.ow[16 * y + k:16 * y + 16:2, 0:512], T.hl[:, 256 * k + 32 * y:256 * k + 32 * y + 32],
+                              ["hl%d" % k, "xs"], ["ow0"]) for k in range(2) for y in range(8)])
+            elif s[0] == "i":
+                inv_part(e, t, int(s[1]), int(s[2]))
+            else:
+                late_const(e, int(s[1]))
+
+    def inv_part(e, t, a, b):
+        old, new = "inv%d" % ((t - 1) % 2), "inv%d" % (t % 2)
+        gather(e, T[new][:, 512 * a:512 * b], T[old][:, 0:4096], T.lf[:, 256 * t + 32 * a:256 * t + 32 * b],
+               quarters(old) + ["lf%d" % t], quarters(new)[a:b])
+
+    def inv_wrap(t, q):
+        name = "inv%d" % (t % 2)
+        wrap("pw", 64 * q, T[name], quarters(name)[2 * q:2 * q + 2], "zo", 64 * q, 64)
+
+    def shifts(t):
+        c = 64 * t
+        if t > 0:
+            inv_part("S", t, 2, 5)
+        else:
+            late_const("S", 1)
+            late_const("S", 2)
+        for a in range(4):
+            out = T.pk[32 * a:32 * a + 32, 0:16]
+            mm(out, T.one[0:1, 0:32], T.srow[0:1, 0:16], True, False, ["one", "srow"], ["pk"])
+            mm(out, T.sc[:, 0:32], T.rm[:, 16 * a:16 * a + 16], False, True, ["rm"] + ["sc%d" % k for k in range(32)], ["pk"])
+        for q0 in range(2):
+            op("V", lambda: g.vector.tensor_reduce(T.km[:, q0:q0 + 1], T.pk[:, 8 * q0:8 * q0 + 8], AxisListType.X, A.min),
+               ["pk"], ["km%d" % q0])
+        if t == 0:
+            for k in range(4):
+                q0, sd = k % 2, k // 2
+                op("V", lambda: g.vector.tensor_scalar(T.rh[:, 64 * sd + q0:64 * sd + 64:2], T.mk[:, q0:64:2], T.km[:, q0:q0 + 1],
+                                                       1.0 - 2 * sd, A.mult, A.mult), ["mk0", "km%d" % q0], ["rh%d" % k])
+            mm(T.pk[:, 64:128], T.lh[:, 128:256], T.mk[:, 0:64], True, False, ["lh", "mk0"], ["pk"])
+        else:
+            for q0 in range(2):
+                op("V", lambda: g.vector.tensor_scalar(T.rh[:, 64 * q0:64 * q0 + 64], T.mk[:, c:c + 64], T.km[:, q0:q0 + 1],
+                                                       None, A.mult), ["mk%d" % t, "km%d" % q0], ["rh%d" % q0, "rh%d" % (q0 + 2)])
+        for q0 in range(2):
+            mm(T.pk[:, 64:128], T.lh[:, 128 * q0:128 * q0 + 128], T.rh[:, 64 * q0:64 * q0 + 64], q0 == 0 and t > 0, q0 == 1,
+               ["lh", "rh0", "rh1", "rh2", "rh3"], ["pk"])
+        if t == 0:
+            wrap("pw", 0, T.inv0, quarters("inv0"), "zo", 0, 256)
+        else:
+            inv_wrap(t, 0)
+        op("V", lambda: g.vector.tensor_tensor(T.i1[:], T.pk[:, 64:128], T.cj[:, c:c + 64], A.add), ["pk", "cj%d" % t], ["i1"])
+        op("V", lambda: g.vector.tensor_scalar(T.i2[:], T.i1[:], 7 if t else 224, None, A.bitwise_and), ["i1"], ["i2"])
+        op("V", lambda: g.vector.tensor_tensor(T.i3[:], T.i2[:], T.bs[:, c:c + 64], A.add), ["i2", "bs%d" % t], ["i3"])
+        pc = 1 if t else 2
+        op("V", lambda: g.vector.tensor_scalar(T.rl[:], T.i3[:], T.pf[:, pc:pc + 1], None, A.add), ["i3", "pf%d" % pc], ["rl"])
+        win = T.ow[:, 512 * t:512 * t + 512]
+        n = 1 if t == RO - 1 else 2
+        gather("V", T.bo[:, 0:256 * n], win, T.rl[:, 0:16 * n], ["rl", "ow%d" % t], ["boa"])
+        gather("S", T.bo[:, 256 * n:512 * n], win, T.rl[:, 16 * n:32 * n], ["rl", "ow%d" % t], ["bob"])
+        dmas("tabd", [("YS"[y % 2], T.tab[0:128:8 // n, 512 * y:512 * y + 512], T.bo[16 * y:16 * y + 16, 0:512 * n],
+                       ["boa", "bob"], TABK) for y in range(8)])
+        if t > 0:
+            inv_wrap(t, 1)
+            inv_part("V", t, 5, 6)
+            inv_wrap(t, 2)
+            inv_part("V", t, 6, 7)
+            inv_part("S", t, 7, 8)
+            inv_wrap(t, 3)
+        vcopy(T.li[:], T.pw[:, 0:256], ["pw"], ["li"])
+
+    def conjugate(t):
+        last = t == RO - 1
+        h = HOPS[t]
+        c0, c1 = 256 * t, 256 * (t + 1)
+        fk = ["ft%d" % q for q in range(4)]
+        if last:
+            gather("V", T.ft[:, 0:2048], T.tab[:, 0:4096], T.li[:, 0:128], ["tab", "li"], fk[:2])
+            gather("S", T.ft[:, 2048:4096], T.tab[:, 0:4096], T.li[:, 128:256], ["tab", "li"], fk[2:])
+        else:
+            for q in range(4):
+                gather("VS"[q % 2], T.ft[:, 1024 * q:1024 * q + 1024], T.tab[:, 0:4096], T.li[:, 64 * q:64 * q + 64],
+                       ["tab", "li"], [fk[q]])
+            wrap("pw", 0, T.ft, fk[0:2], "zi", 0, 128)
+        cuts = LAST_CUTS if last else CUTS
+
+        def part(q):
+            v = (LAST_SHARE if last else SHARE)[q]
+            for e, a, b, hf in (("V", 64 * q, 64 * q + v, 0), ("S", 64 * q + v, 64 * q + 64, 1)):
+                gather(e, T.fo[:, 16 * a:16 * b], T.ft[:, 0:4096], T.lr[:, c0 + a:c0 + b],
+                       fk + ["lr%d" % t], ["fo%d%s" % (q, "ab"[hf])])
+
+        def fold(q):
+            k = chunk(cuts, q)
+            wrap("d%d" % k, 64 * (q - cuts[k]), T.fo, ["fo%da" % q, "fo%db" % q], "zo", 64 * q, 64)
+
+        def out(k):
+            a, b = 64 * cuts[k], 64 * cuts[k + 1]
+            key = "sa%d_%d" % (t, k)
+            if last:
+                vcopy(T.ys[:, a:b], T["d%d" % k][:, 0:b - a], ["d%d" % k], [key])
+                send(h, T.yl[:, a:b], T.ys[:, a:b], "a%s%d" % ("ab"[k], t + 1), [key])
+            else:
+                vcopy(T.sa[:, c0 + a:c0 + b], T["d%d" % k][:, 0:b - a], ["d%d" % k], [key])
+                send(h, T.lo[:, c1 + a:c1 + b], T.sa[:, c0 + a:c0 + b], "a%s%d" % ("abc"[k], t + 1), [key])
+
+        if last:
+            for q in range(4):
+                part(q)
+                fold(q)
+            out(0)
+            out(1)
+            dmas("st", [("Y", T.yo[:, 0:192], T.yl[:, 0:192], ["loa%d" % RO], []),
+                        ("S", T.yo[:, 192:256], T.yl[:, 192:256], ["lob%d" % RO], [])])
+            return
+        wrap("pw", 128, T.ft, fk[2:4], "zi", 128, 128)
+        part(0)
+        fold(0)
+        part(1)
+        fold(1)
+        out(0)
+        vcopy(T.sf[:, c0:c0 + 256], T.pw[:, 0:256], ["pw"], ["sf%d" % t])
+        send(h, T.lf[:, c1:c1 + 256], T.sf[:, c0:c0 + 256], "af%d" % (t + 1), ["sf%d" % t])
+        part(2)
+        fold(2)
+        out(1)
+        part(3)
+        fold(3)
+        out(2)
+        window_dmas(T.so, 512 * t, "so%d" % t, range(8))
+        send(h - HOPS[t + 1], T.lr[:, c1:c1 + 256], T.sa[:, c0:c0 + 256], "ar%d" % (t + 1), ["sa%d_%d" % (t, k) for k in range(3)])
+        send(h, T.ow[:, 512 * (t + 1):512 * (t + 2)], T.so[:, 512 * t:512 * t + 512], "ao%d" % (t + 1), ["so%d" % t])
+        if t + 2 < RO:
+            round_consts(t + 2)
+
+    round_consts(1)
+    for t in range(RO):
+        scores(t)
+        shifts(t)
+        conjugate(t)
+    for s in count:
+        wait("G", (s, count[s]))

@@ -5,7 +5,7 @@ HOPS = (1, 2, 3, 4, 5, 6)
 N = 8
 
 SCRATCH = {
-    "xs": ("sbuf", [128, 4096], "bfloat16"),
+    "xs": ("sbuf", [128, RO * 4096], "bfloat16"),
     "xo": ("sbuf", [128, 4096], "bfloat16"),
     "xt": ("sbuf", [128, 4096], "bfloat16"),
     "tab": ("sbuf", [128, 4096], "bfloat16"),
@@ -18,11 +18,10 @@ SCRATCH = {
     "lo": ("sbuf", [128, RO * 256], "uint16"),
     "lr": ("sbuf", [128, RO * 256], "uint16"),
     "lf": ("sbuf", [128, RO * 256], "uint16"),
-    "sa": ("sbuf", [128, RO * 256], "uint16"),
-    "sf": ("sbuf", [128, RO * 256], "uint16"),
+    "isn": ("sbuf", [128, RO * 512], "bfloat16"),
+    "ir": ("sbuf", [128, RO * 512], "bfloat16"),
     "li": ("sbuf", [128, 256], "uint16"),
     "ow": ("sbuf", [128, RO * 512], "bfloat16"),
-    "so": ("sbuf", [128, RO * 512], "bfloat16"),
     "bo": ("sbuf", [128, 1024], "bfloat16"),
     "ys": ("sbuf", [128, 256], "float32"),
     "yl": ("sbuf", [128, 256], "float32"),
@@ -60,20 +59,24 @@ SCRATCH = {
     "pw": ("psum", [128, 512], "float32"),
     "pk": ("psum", [128, 512], "float32"),
 }
-SEMAPHORES = (["cV", "cS", "cP", "cG", "ldo", "ldx", "iot", "tabd", "owd", "sent", "st"]
-              + ["%s%d" % (n, t) for n in ("aa", "ab", "ac", "ar", "af", "ao") for t in range(RO + 1)])
+SEMAPHORES = (["cV", "cS", "cP", "cG", "ldo", "ldx", "tabd", "owd", "pack", "unp", "sent", "st", "aa", "ab"]
+              + ["%s%d" % (n, t) for n in ("ar", "ax", "ai") for t in range(RO)])
 PSUM = ("d0", "d1", "d2", "d3", "t0", "t1", "pw", "pk")
 
-V_SEQ = "ga0 ga1 e0 i01 r0 ga2 e1 r0 r0 r1 e2 r1 r1 ga3 r1 r2 e3 r2 r2 r2 r3 r3 r3".split()
-S_SEQ = "gb0 gb1 i12 r0 r0 gb2 r0 r0 r0 r1 r1 r1 r1 gb3 r2 r2 r2 r2 r3 r3 r3 r3 r3".split()
-V_SEQ0 = "s0 s1 u0 s2 s3 e0 s4 r0 e1 e2 r0 s5 r0 e3 r2 s6 r2 r2 r2 s7 r2 r2 r3 r3 r3".split()
-S_SEQ0 = "ga0 gb0 c0 gb1 ga1 ga2 r0 gb2 gb3 r0 r0 ga3 r0 r0 r1 r1 r1 c3 r1 r1 r1 r1 r1 r2 r2 r3 r3 r3 r3 r3".split()
-COST = {"g": 0.9, "e": 0.6, "r": 0.62, "s": 2.05, "u": 1.0, "c": 0.6, "i": 0.9}
+V_SEQ = "ga0 ga1 o1 e0 ga2 r0 o2 e1 r0 r0 r1 e2 r1 r1 ga3 r2 r2 e3 r2 r2 r2 r3 r3 r3 i01".split()
+S_SEQ = "gb0 gb1 gb2 r0 r0 r0 r0 r0 r1 r1 r1 r1 gb3 r1 r2 r2 r2 r3 r3 r3 r3 r3".split()
+V_SEQ0 = "s0 s1 s2 u0 s3 e0 s4 e1 e2 r0 s5 r0 r1 e3 r2 r2 s6 r2 r2 r2 r2 r2 r3 r3 r3".split()
+S_SEQ0 = "ga0 gb0 c0 ga1 gb1 ga2 r0 gb2 r0 r0 r0 ga3 gb3 r0 r0 r1 r1 c3 r1 r1 r1 r1 r1 r2 r3 r3 r3 r3 r3".split()
+COST = {"g": 0.9, "e": 0.6, "r": 0.62, "s": 2.05, "u": 1.0, "c": 0.6, "i": 0.9, "o": 0.3}
 
 
 TABK = ["tab", "tab1", "tab2", "tab3"]
 BIG64 = 1.5 * 2.0 ** 29
-CUTS = (0, 1, 2, 4)
+INV_MID, INV_END = 1, 4
+INV_POST = (("V", 4, 6), ("S", 6, 8))
+F_SHARE = (60, 60)
+O_SHARE = (64, 60)
+CUTS = (0, 2, 4)
 LAST_CUTS = (0, 3, 4)
 SHARE = (32, 32, 26, 26)
 LAST_SHARE = (32, 32, 32, 32)
@@ -214,19 +217,16 @@ def rank_program(g, core, T, topo):
     def quarters(name):
         return ["%s%d%s" % (name, q, h) for q in range(4) for h in "ab"]
 
-    arrives("lr0", "ar0", from_(-1))
-    for t in range(1, RO + 1):
-        h = HOPS[t - 1]
-        arrives("loa%d" % t, "aa%d" % t, from_(h))
-        arrives("lob%d" % t, "ab%d" % t, from_(h))
-        if t < RO:
-            arrives("loc%d" % t, "ac%d" % t, from_(h))
-            arrives("lr%d" % t, "ar%d" % t, from_(h - HOPS[t]))
-            arrives("lf%d" % t, "af%d" % t, from_(h))
-            arrives("ow%d" % t, "ao%d" % t, from_(h))
+    for t in range(RO):
+        arrives("lr%d" % t, "ar%d" % t, from_(-HOPS[t]))
+        if t > 0:
+            arrives("xs%d" % t, "ax%d" % t, from_(-sum(HOPS[:t])))
+            arrives("ir%d" % t, "ai%d" % t, from_(-HOPS[t - 1]))
+    arrives("yla", "aa", from_(sum(HOPS)))
+    arrives("ylb", "ab", from_(sum(HOPS)))
 
     dmas("ldo", [("Y", T.oi[:], T.o[:], [], ["oi"])])
-    dmas("ldx", [("S", T.xs[:], T.x[:], [], ["xs"])])
+    dmas("ldx", [("S", T.xs[:, 0:4096], T.x[:], [], ["xs0"])])
     iota(T.pi[:, 0:1], [[0, 1]], 0, 1, "pi", False)
     iota(T.ramp[:], [[1, 64]], 0, 0, "ramp")
     memset(T.idn[:], 0.0, "idn")
@@ -246,6 +246,7 @@ def rank_program(g, core, T, topo):
         n = 512 << k
         op("S", lambda: g.scalar.activation(T.tab[:, n:2 * n], T.tab[:, 0:n], AF.Identity, bias=T.hc[:, n // 64:n // 64 + 1]),
            ["tab", "hc"] + TABK[1:k + 1], [TABK[k + 1]])
+    op("S", lambda: g.scalar.activation(T.ft[:, 3584:4096], T.tab[:, 0:512], AF.Identity, bias=T.hc[:, 56:57]), ["tab", "hc"], ["ft3"])
     vcopy(T.lo[:, 0:256], T.oi[:], ["oi"], ["loa0", "lob0", "loc0"])
     sel(T.idn[:], [[-1, 128]], A.not_equal, 1.0, 0, 1, "idn")
     d3 = T.dm[64:128, 1536:2048]
@@ -319,6 +320,13 @@ def rank_program(g, core, T, topo):
         dmas("owd", [("Y", dst[16 * y:16 * y + 16, col:col + 512], T.fo[0:128:8, 512 * y:512 * y + 512],
                       ["fo%da" % (y // 2), "fo%db" % (y // 2)], [key]) for y in gs])
 
+    later = {}
+
+    def scatter(q):
+        src, key = (T.ft, "ft3") if q == 7 else (T.tab, TABK[q.bit_length()])
+        op("V", lambda: g.vector.tensor_copy(T.inv0[:, 0:4096].indirect(T.lo[:, 32 * q:32 * q + 32]),
+                                             src[:, 512 * q:512 * q + 512]), [key, "lob0"], quarters("inv0"))
+
     def scores(t):
         vs, ss = (V_SEQ0, S_SEQ0) if t == 0 else (V_SEQ, S_SEQ)
         c0 = 256 * t
@@ -337,7 +345,8 @@ def rank_program(g, core, T, topo):
                 if pos[e] < len(seq[e]):
                     s = seq[e][pos[e]]
                     q = s[-1]
-                    need = {"e": ["ga" + q, "gb" + q], "r": ["e" + q] + (["c0"] if t == 0 else [])}.get(s[0], [])
+                    need = {"e": ["ga" + q, "gb" + q], "r": ["e" + q] + (["c0"] if t == 0 else []),
+                            "i": ["o2"], "g": ["o1"] if t and chunk(CUTS, int(q)) else []}.get(s[0], [])
                     if all(k in ready for k in need):
                         cand.append((max([clock[e]] + [ready[k] + 0.6 for k in need]), e, s, need))
             at, e, s, need = min(cand)
@@ -366,8 +375,8 @@ def rank_program(g, core, T, topo):
             if s[0] == "g":
                 q, hf = int(s[2]), "ab".index(s[1])
                 a = 64 * q + 32 * hf
-                gather(e, T.xo[:, 16 * a:16 * a + 512], T.xs[:, 0:4096], T.lo[:, c0 + a:c0 + a + 32],
-                       ["xs", "lo%s%d" % ("abc"[chunk(CUTS, q)], t)], ["xo%d%s" % (q, s[1])])
+                gather(e, T.xo[:, 16 * a:16 * a + 512], T.xs[:, 4096 * t:4096 * t + 4096], T.lo[:, c0 + a:c0 + a + 32],
+                       ["xs%d" % t, "lo%s%d" % ("abc"[chunk(CUTS, q)], t)], ["xo%d%s" % (q, s[1])])
             elif s == "t":
                 tb = "t%d" % (n % 2)
                 for b in range(8):
@@ -402,16 +411,17 @@ def rank_program(g, core, T, topo):
                     op(e, lambda: g.scalar.activation(T.junk[:, j:j + 512], T[bank][:, 0:512], AF.Abs,
                                                       accum_out=T.sc[:, col:col + 1]), [bank], ["sc%d" % col, "junk%d" % (n % 8)])
             elif s[0] == "s":
-                q = int(s[1])
-                op(e, lambda: g.vector.tensor_copy(T.inv0[:, 0:4096].indirect(T.lo[:, 32 * q:32 * q + 32]),
-                                                   T.tab[:, 512 * q:512 * q + 512]),
-                   [TABK[q.bit_length()], "lob0"], quarters("inv0"))
+                scatter(int(s[1]))
             elif s[0] == "u":
                 op(e, lambda: g.vector.tensor_scalar(T.hl[:, 0:256], T.oi[:], BIG64, -BIG64, A.add, A.add), ["oi"], ["hl0"])
                 op(e, lambda: g.vector.tensor_tensor(T.hl[:, 256:512], T.oi[:], T.hl[:, 0:256], A.subtract), ["oi", "hl0"], ["hl1"])
                 op(e, lambda: g.vector.tensor_scalar(T.pf[:, 2:3], T.pf[:, 0:1], 32.0, None, A.mult), ["pf0"], ["pf2"])
                 dmas("owd", [("Y", T.ow[16 * y + k:16 * y + 16:2, 0:512], T.hl[:, 256 * k + 32 * y:256 * k + 32 * y + 32],
-                              ["hl%d" % k, "xs"], ["ow0"]) for k in range(2) for y in range(8)])
+                              ["hl%d" % k, "xs0"], ["ow0"]) for k in range(2) for y in range(8)])
+            elif s[0] == "o":
+                later[s]()
+                if s == "o1":
+                    later["rest"]()
             elif s[0] == "i":
                 inv_part(e, t, int(s[1]), int(s[2]))
             else:
@@ -424,12 +434,12 @@ def rank_program(g, core, T, topo):
 
     def inv_wrap(t, q):
         name = "inv%d" % (t % 2)
-        wrap("pw", 64 * q, T[name], quarters(name)[2 * q:2 * q + 2], "zo", 64 * q, 64)
+        wrap(("pw", "d0")[q // 2], 64 * (q % 2), T[name], quarters(name)[2 * q:2 * q + 2], "zo", 64 * q, 64)
 
     def shifts(t):
         c = 64 * t
         if t > 0:
-            inv_part("S", t, 2, 5)
+            inv_part("S", t, INV_MID, INV_END)
         else:
             late_const("S", 1)
             late_const("S", 2)
@@ -453,9 +463,7 @@ def rank_program(g, core, T, topo):
         for q0 in range(2):
             mm(T.pk[:, 64:128], T.lh[:, 128 * q0:128 * q0 + 128], T.rh[:, 64 * q0:64 * q0 + 64], q0 == 0 and t > 0, q0 == 1,
                ["lh", "rh0", "rh1", "rh2", "rh3"], ["pk"])
-        if t == 0:
-            wrap("pw", 0, T.inv0, quarters("inv0"), "zo", 0, 256)
-        else:
+        if t > 0:
             inv_wrap(t, 0)
         op("V", lambda: g.vector.tensor_tensor(T.i1[:], T.pk[:, 64:128], T.cj[:, c:c + 64], A.add), ["pk", "cj%d" % t], ["i1"])
         op("V", lambda: g.vector.tensor_scalar(T.i2[:], T.i1[:], 7 if t else 224, None, A.bitwise_and), ["i1"], ["i2"])
@@ -469,26 +477,33 @@ def rank_program(g, core, T, topo):
         dmas("tabd", [("YS"[y % 2], T.tab[0:128:8 // n, 512 * y:512 * y + 512], T.bo[16 * y:16 * y + 16, 0:512 * n],
                        ["boa", "bob"], TABK) for y in range(8)])
         if t > 0:
+            for e, a, b in INV_POST:
+                inv_part(e, t, a, b)
             inv_wrap(t, 1)
-            inv_part("V", t, 5, 6)
             inv_wrap(t, 2)
-            inv_part("V", t, 6, 7)
-            inv_part("S", t, 7, 8)
             inv_wrap(t, 3)
-        vcopy(T.li[:], T.pw[:, 0:256], ["pw"], ["li"])
+        else:
+            scatter(7)
+            wrap("pw", 0, T.inv0, quarters("inv0"), "zo", 0, 128)
+            wrap("d0", 0, T.inv0, quarters("inv0"), "zo", 128, 128)
+        if t < RO - 1:
+            name = "inv%d" % (t % 2)
+            dmas("pack", [("Y", T.isn[:, 512 * t:512 * t + 512], T[name][0:128:8, :], quarters(name), ["isn%d" % t])])
+            send(-HOPS[t], T.ir[:, 512 * (t + 1):512 * (t + 2)], T.isn[:, 512 * t:512 * t + 512], "ai%d" % (t + 1), ["isn%d" % t])
+        vcopy(T.li[:, 0:128], T.pw[:, 0:128], ["pw"], ["li0"])
 
     def conjugate(t):
         last = t == RO - 1
         h = HOPS[t]
         c0, c1 = 256 * t, 256 * (t + 1)
         fk = ["ft%d" % q for q in range(4)]
-        if last:
-            gather("V", T.ft[:, 0:2048], T.tab[:, 0:4096], T.li[:, 0:128], ["tab", "li"], fk[:2])
-            gather("S", T.ft[:, 2048:4096], T.tab[:, 0:4096], T.li[:, 128:256], ["tab", "li"], fk[2:])
-        else:
-            for q in range(4):
-                gather("VS"[q % 2], T.ft[:, 1024 * q:1024 * q + 1024], T.tab[:, 0:4096], T.li[:, 64 * q:64 * q + 64],
-                       ["tab", "li"], [fk[q]])
+        for hf in range(2):
+            a, m, b = 128 * hf, 128 * hf + F_SHARE[hf], 128 * hf + 128
+            gather("V", T.ft[:, 16 * a:16 * m], T.tab[:, 0:4096], T.li[:, a:m], ["tab", "li%d" % hf], [fk[2 * hf]])
+            gather("S", T.ft[:, 16 * m:16 * b], T.tab[:, 0:4096], T.li[:, m:b], ["tab", "li%d" % hf], [fk[2 * hf + 1]])
+            if hf == 0:
+                vcopy(T.li[:, 128:256], T.d0[:, 0:128], ["d0"], ["li1"])
+        if not last:
             wrap("pw", 0, T.ft, fk[0:2], "zi", 0, 128)
         cuts = LAST_CUTS if last else CUTS
 
@@ -504,13 +519,11 @@ def rank_program(g, core, T, topo):
 
         def out(k):
             a, b = 64 * cuts[k], 64 * cuts[k + 1]
-            key = "sa%d_%d" % (t, k)
             if last:
-                vcopy(T.ys[:, a:b], T["d%d" % k][:, 0:b - a], ["d%d" % k], [key])
-                send(h, T.yl[:, a:b], T.ys[:, a:b], "a%s%d" % ("ab"[k], t + 1), [key])
+                vcopy(T.ys[:, a:b], T["d%d" % k][:, 0:b - a], ["d%d" % k], ["ys%d" % k])
+                send(sum(HOPS), T.yl[:, a:b], T.ys[:, a:b], "a" + "ab"[k], ["ys%d" % k])
             else:
-                vcopy(T.sa[:, c0 + a:c0 + b], T["d%d" % k][:, 0:b - a], ["d%d" % k], [key])
-                send(h, T.lo[:, c1 + a:c1 + b], T.sa[:, c0 + a:c0 + b], "a%s%d" % ("abc"[k], t + 1), [key])
+                vcopy(T.lo[:, c1 + a:c1 + b], T["d%d" % k][:, 0:b - a], ["d%d" % k], ["lo%s%d" % ("abc"[k], t + 1)])
 
         if last:
             for q in range(4):
@@ -518,29 +531,34 @@ def rank_program(g, core, T, topo):
                 fold(q)
             out(0)
             out(1)
-            dmas("st", [("Y", T.yo[:, 0:192], T.yl[:, 0:192], ["loa%d" % RO], []),
-                        ("S", T.yo[:, 192:256], T.yl[:, 192:256], ["lob%d" % RO], [])])
+            dmas("st", [("Y", T.yo[:, 0:192], T.yl[:, 0:192], ["yla"], []),
+                        ("S", T.yo[:, 192:256], T.yl[:, 192:256], ["ylb"], [])])
             return
+        dmas("unp", [("Y", T["inv%d" % (t % 2)][0:128:8, :], T.ir[:, 512 * (t + 1):512 * (t + 2)], ["ir%d" % (t + 1)],
+                      quarters("inv%d" % (t % 2)))])
         wrap("pw", 128, T.ft, fk[2:4], "zi", 128, 128)
-        part(0)
-        fold(0)
-        part(1)
-        fold(1)
+        for hf in range(2):
+            a, m, b = 128 * hf, 128 * hf + O_SHARE[hf], 128 * hf + 128
+            ka, kb = ["fo%da" % (2 * hf), "fo%db" % (2 * hf)], ["fo%da" % (2 * hf + 1), "fo%db" % (2 * hf + 1)]
+            gather("V", T.fo[:, 16 * a:16 * m], T.ft[:, 0:4096], T.lr[:, c0 + a:c0 + m], fk + ["lr%d" % t], [ka[0], kb[0]])
+            gather("S", T.fo[:, 16 * m:16 * b], T.ft[:, 0:4096], T.lr[:, c0 + m:c0 + b], fk + ["lr%d" % t], [ka[1], kb[1]])
+            wrap("d%d" % hf, 0, T.fo, ka + kb, "zo", a, 128)
         out(0)
-        vcopy(T.sf[:, c0:c0 + 256], T.pw[:, 0:256], ["pw"], ["sf%d" % t])
-        send(h, T.lf[:, c1:c1 + 256], T.sf[:, c0:c0 + 256], "af%d" % (t + 1), ["sf%d" % t])
-        part(2)
-        fold(2)
-        out(1)
-        part(3)
-        fold(3)
-        out(2)
-        window_dmas(T.so, 512 * t, "so%d" % t, range(8))
-        send(h - HOPS[t + 1], T.lr[:, c1:c1 + 256], T.sa[:, c0:c0 + 256], "ar%d" % (t + 1), ["sa%d_%d" % (t, k) for k in range(3)])
-        send(h, T.ow[:, 512 * (t + 1):512 * (t + 2)], T.so[:, 512 * t:512 * t + 512], "ao%d" % (t + 1), ["so%d" % t])
-        if t + 2 < RO:
-            round_consts(t + 2)
+        window_dmas(T.ow, 512 * (t + 1), "ow%d" % (t + 1), range(8))
+        later["o1"] = lambda: out(1)
+        later["o2"] = lambda: vcopy(T.lf[:, c1:c1 + 256], T.pw[:, 0:256], ["pw"], ["lf%d" % (t + 1)])
 
+        def rest():
+            send(-HOPS[t + 1], T.lr[:, c1:c1 + 256], T.lo[:, c1:c1 + 256], "ar%d" % (t + 1), ["loa%d" % (t + 1), "lob%d" % (t + 1)])
+            if t + 2 < RO:
+                send_x(t + 2)
+                round_consts(t + 2)
+        later["rest"] = rest
+
+    def send_x(t):
+        send(-sum(HOPS[:t]), T.xs[:, 4096 * t:4096 * t + 4096], T.xs[:, 0:4096], "ax%d" % t, ["xs0"])
+
+    send_x(1)
     round_consts(1)
     for t in range(RO):
         scores(t)

@@ -1,89 +1,106 @@
+from concourse.bass import DstId, RemoteDMATransfer
 from concourse.mybir import AluOpType, AxisListType, ActivationFunctionType
 
 RO = 6
 HOPS = (1, 2, 3, 4, 5, 6)
 N = 8
+ND = (5, 3, 3, 3, 3, 3)
+DUP = 128 * 7
+H1 = 2048 + DUP
 
 SCRATCH = {
     "xs": ("sbuf", [128, RO * 4096], "bfloat16"),
-    "xo": ("sbuf", [128, 4096], "bfloat16"),
-    "xt": ("sbuf", [128, 4096], "bfloat16"),
+    "xo": ("sbuf", [128, H1 + 2048], "bfloat16"),
+    "xt": ("sbuf", [128, 2048], "bfloat16"),
+    "ml": ("sbuf", [128, 8 * 1024], "bfloat16"),
+    "mp": ("sbuf", [128, sum(ND) * 1024], "bfloat16"),
     "tab": ("sbuf", [128, 4096], "bfloat16"),
     "ft": ("sbuf", [128, 4096], "bfloat16"),
     "fo": ("sbuf", [128, 4096], "bfloat16"),
     "inv0": ("sbuf", [128, 4096], "bfloat16"),
     "inv1": ("sbuf", [128, 4096], "bfloat16"),
-    "junk": ("sbuf", [128, 4096], "bfloat16"),
+    "junk": ("sbuf", [128, 1024], "bfloat16"),
     "oi": ("sbuf", [128, 256], "int32"),
-    "lo": ("sbuf", [128, RO * 256], "uint16"),
+    "ln": ("sbuf", [128, 256], "uint16"),
+    "lx": ("sbuf", [128, 256], "uint16"),
+    "ls": ("sbuf", [128, RO * 256], "uint16"),
     "lr": ("sbuf", [128, RO * 256], "uint16"),
-    "lf": ("sbuf", [128, RO * 256], "uint16"),
-    "isn": ("sbuf", [128, RO * 512], "bfloat16"),
-    "ir": ("sbuf", [128, RO * 512], "bfloat16"),
+    "lf": ("sbuf", [128, 256], "uint16"),
     "li": ("sbuf", [128, 256], "uint16"),
-    "ow": ("sbuf", [128, RO * 512], "bfloat16"),
+    "isn": ("sbuf", [128, 5 * 1024], "bfloat16"),
+    "ir": ("sbuf", [128, 5 * 1024], "bfloat16"),
+    "ow": ("sbuf", [128, 2 * 1024], "bfloat16"),
     "bo": ("sbuf", [128, 1024], "bfloat16"),
     "ys": ("sbuf", [128, 256], "float32"),
     "yl": ("sbuf", [128, 256], "float32"),
-    "dm": ("sbuf", [128, 4 * 512], "bfloat16"),
-    "pm": ("sbuf", [128, 3 * 128], "bfloat16"),
+    "dm": ("sbuf", [128, 1024], "bfloat16"),
+    "pm": ("sbuf", [128, 128], "bfloat16"),
     "idn": ("sbuf", [128, 128], "bfloat16"),
-    "zo": ("sbuf", [128, 144], "bfloat16"),
-    "zi": ("sbuf", [128, 144], "bfloat16"),
-    "rm": ("sbuf", [128, 64], "float32"),
-    "lht": ("sbuf", [128, 256], "bfloat16"),
-    "lh": ("sbuf", [128, 256], "float32"),
-    "mk": ("sbuf", [128, RO * 64], "float32"),
-    "cj": ("sbuf", [128, RO * 64], "float32"),
-    "bs": ("sbuf", [128, RO * 64], "float32"),
-    "one": ("sbuf", [128, 32], "bfloat16"),
-    "srow": ("sbuf", [128, 16], "bfloat16"),
-    "pi": ("sbuf", [128, 4], "int32"),
-    "pf": ("sbuf", [128, 4], "float32"),
+    "zz": ("sbuf", [128, 7 * 144], "bfloat16"),
+    "cf": ("sbuf", [128, 576], "float32"),
+    "row": ("sbuf", [128, 512], "float32"),
+    "one": ("sbuf", [128, 128], "bfloat16"),
+    "srow": ("sbuf", [128, 32], "bfloat16"),
+    "base": ("sbuf", [128, 128], "float32"),
+    "pi": ("sbuf", [128, 8], "int32"),
+    "mk": ("sbuf", [128, 4], "float32"),
     "hl": ("sbuf", [128, 512], "bfloat16"),
-    "ramp": ("sbuf", [128, 64], "float32"),
-    "hc": ("sbuf", [128, 64], "float32"),
-    "sc": ("sbuf", [128, 32], "float32"),
+    "ramp": ("sbuf", [128, 8], "float32"),
+    "hc": ("sbuf", [128, 8], "float32"),
+    "kl": ("sbuf", [128, 8], "float32"),
+    "ks": ("sbuf", [128, RO * 8], "float32"),
+    "kr": ("sbuf", [128, RO * 8], "float32"),
     "km": ("sbuf", [128, 4], "float32"),
-    "rh": ("sbuf", [128, 128], "float32"),
-    "i1": ("sbuf", [128, 64], "int32"),
-    "i2": ("sbuf", [128, 64], "int32"),
-    "i3": ("sbuf", [128, 64], "float32"),
     "rl": ("sbuf", [128, 64], "uint16"),
     "d0": ("psum", [128, 512], "float32"),
     "d1": ("psum", [128, 512], "float32"),
     "d2": ("psum", [128, 512], "float32"),
-    "d3": ("psum", [128, 512], "float32"),
-    "t0": ("psum", [128, 1024], "bfloat16"),
-    "t1": ("psum", [128, 1024], "bfloat16"),
-    "pw": ("psum", [128, 512], "float32"),
+    "tb": ("psum", [128, 1024], "bfloat16"),
+    "pa": ("psum", [128, 1024], "float32"),
+    "pl": ("psum", [128, 512], "float32"),
     "pk": ("psum", [128, 512], "float32"),
 }
-SEMAPHORES = (["cV", "cS", "cP", "cG", "ldo", "ldx", "tabd", "owd", "pack", "unp", "sent", "st", "aa", "ab"]
-              + ["%s%d" % (n, t) for n in ("ar", "ax", "ai") for t in range(RO)])
-PSUM = ("d0", "d1", "d2", "d3", "t0", "t1", "pw", "pk")
-
-V_SEQ = "ga0 ga1 o1 e0 ga2 r0 o2 e1 r0 r0 r1 e2 r1 r1 ga3 r2 r2 e3 r2 r2 r2 r3 r3 r3 i01".split()
-S_SEQ = "gb0 gb1 gb2 r0 r0 r0 r0 r0 r1 r1 r1 r1 gb3 r1 r2 r2 r2 r3 r3 r3 r3 r3".split()
-V_SEQ0 = "s0 s1 s2 u0 s3 e0 s4 e1 e2 r0 s5 r0 r1 e3 r2 r2 s6 r2 r2 r2 r2 r2 r3 r3 r3".split()
-S_SEQ0 = "ga0 gb0 c0 ga1 gb1 ga2 r0 gb2 r0 r0 r0 ga3 gb3 r0 r0 r1 r1 c3 r1 r1 r1 r1 r1 r2 r3 r3 r3 r3 r3".split()
-COST = {"g": 0.9, "e": 0.6, "r": 0.62, "s": 2.05, "u": 1.0, "c": 0.6, "i": 0.9, "o": 0.3}
-
-
-TABK = ["tab", "tab1", "tab2", "tab3"]
+SEMAPHORES = (["cV", "cS", "cP", "cG", "ldo", "ldx", "tabd", "owd", "owe", "pack", "unp", "sent", "sf", "st", "ay", "fst", "late"]
+              + ["%s%d" % (n, t) for n in ("ar", "ax", "ai", "ak") for t in range(RO)]
+              + ["af%d_%d" % (t, s) for t in range(RO) for s in range(ND[t])])
+PSUM = ("d0", "d1", "d2", "tb", "pa", "pl", "pk")
 BIG64 = 1.5 * 2.0 ** 29
-INV_MID, INV_END = 1, 4
-INV_POST = (("V", 4, 6), ("S", 6, 8))
-F_SHARE = (60, 60)
-O_SHARE = (64, 60)
-CUTS = (0, 2, 4)
-LAST_CUTS = (0, 3, 4)
-SHARE = (32, 32, 26, 26)
-LAST_SHARE = (32, 32, 32, 32)
+
+Y, J = ["y2", "y1", "y0"], ["j2", "j1", "j0"]
+FIELDS = (["b1", "b0"], ["b5", "b2"], ["b4", "b3"])
+ROLES = ((0, 2, 1), (0, 2, 1), (1, 0, 2), (2, 0, 1), (2, 0, 1), (1, 0, 2))
+NATURAL = Y + ["b5", "b4", "b3", "b2", "b1", "b0"] + J
+FIRST = ["y2", "b0"] + J + ["y1", "y0", "b5", "b4", "b3", "b2", "b1"]
+STAR = Y + J + ["b0", "b5", "b4", "b3", "b2", "b1"]
+LAST = J + ["b1", "b0", "b2"] + Y + ["b5", "b4", "b3"]
 
 
-def chunk(cuts, q):
-    return max(k for k in range(len(cuts) - 1) if cuts[k] <= q)
+def roles(t):
+    f, u, v = (FIELDS[k] for k in ROLES[t])
+    side = "b%d" % t
+    q = [b for b in f if b != side][0]
+    if t == 0:
+        return side, q, ["b3", "b2"], ["b4", "b5"], u + v
+    return side, q, u, v, u + v
+
+
+def order(t):
+    if t == RO - 1:
+        return LAST
+    side, q, a, c, r = roles(t + 1)
+    return Y + J + a + [q, side] + c
+
+
+def wt(bits):
+    return {b: 1 << (len(bits) - 1 - k) for k, b in enumerate(bits)}
+
+
+def values(bits):
+    return [{b: n >> (len(bits) - 1 - k) & 1 for k, b in enumerate(bits)} for n in range(1 << len(bits))]
+
+
+def dot(w, v):
+    return sum(w[b] * v[b] for b in v if b in w)
 
 
 def pieces(weights):
@@ -105,7 +122,20 @@ def pieces(weights):
     return out
 
 
-CODE_W = ([0, 4, 8, 1, 2], [0, 4, 8, 1, 2], [4, 0, 8, 1, 2], [4, 8, 0, 1, 2], [4, 8, 1, 0, 2], [4, 8, 1, 2, 0])
+SEQ = {"V": "g8:9 x0 e0:1 g0:4 u e1:2 g12:14 m3 e2:3 g14:16 m4 e3:4 m5 lf m6 m7 i0:1 kl i1:3",
+       "S": "g9:10 g10:12 g4:8 r0 r1 r2 r3 r4 r5 r6 r7 r8 r9 r10 r11 kp r12 r13 r14 r15",
+       "G": "f0 f1 f2 K"}
+SEQ0 = {"V": "s0 s1 x0 e0:1 g0:3 s2 u e1:2 s3 e2:3 s4 e3:4 m5 m6 m7 s5 kl s6",
+        "S": "g8:10 g10:12 c0 g3:8 r0 r1 r2 g12:14 r3 o r4 r5 g14:16 r6 r7 r8 cb r9 r10 r11 r12 kp r13 r14 r15",
+        "G": "G0 G1 G2 G3 f0 f1 f2 f3 f4 G4 K G5"}
+COST = {"g": 0.39, "u": 0.2, "x": 0.18, "e": 0.27, "r": 0.55, "m": 1.05, "k": 0.1, "i": 0.39, "l": 0.3, "s": 1.85, "c": 0.4,
+        "o": 1.1, "f": 0.3, "K": 0.3, "G": 1.3}
+START = (4.0, 5.3, 5.1, 6.0)
+FOLD, HOP = 1.6, 2.0
+LATE = 7
+INV_PRE, INV_MID = 3, 5
+INV_POST = (("V", 5, 8), ("S", 8, 13), ("V", 13, 16))
+F_SHARE = (60, 60)
 
 
 def rank_program(g, core, T, topo):
@@ -172,18 +202,17 @@ def rank_program(g, core, T, topo):
     def peer(d):
         return T.cores[(rank + d) % N]
 
-    def width(dst):
-        return len(topo.engines(core, dst))
+    near = [c for c in T.cores if topo.chip(c) == topo.chip(core) and topo.die(c) == topo.die(core)]
+    partner = near[near.index(core) ^ 1]
 
-    def send(d, out, in_, sem, rd):
-        dst = peer(d)
+    def width(src, dst):
+        return len(topo.engines(src, dst))
+
+    def send(dst, out, in_, sem, rd):
         deps("G", rd, ())
         rid, pid, _ = topo.addr(dst)
         g.remote_dma(out, in_, T.sem[sem], T.sem.sent, pid, rid, topo.mask(core, dst))
-        count["sent"] = count.get("sent", 0) + width(dst)
-
-    def from_(d):
-        return len(topo.engines(peer(-d), core))
+        count["sent"] = count.get("sent", 0) + width(core, dst)
 
     def gather(e, out, win, off, rd, wr):
         if e == "V":
@@ -194,8 +223,8 @@ def rank_program(g, core, T, topo):
     def mm(out, lhsT, rhs, start, stop, rd, wr):
         op("P", lambda: g.tensor.matmul(out, lhsT, rhs, start, stop), rd, wr)
 
-    def sel(ap, pat, cmp, fill, base, cm, key):
-        op("G", lambda: g.affine_select(ap, ap, pat, cmp, fill, base, cm), [key], [key])
+    def sel(ap, pat, fill, base, key, cm=1):
+        op("G", lambda: g.affine_select(ap, ap, pat, A.not_equal, fill, base, cm), [key], [key])
 
     def iota(ap, pat, base, cm, key, small=True):
         if small:
@@ -203,363 +232,493 @@ def rank_program(g, core, T, topo):
         else:
             op("G", lambda: g.iota(ap, pat, base, cm), [], [key])
 
-    def memset(ap, v, key):
-        op("V", lambda: g.vector.memset(ap, v), [], [key])
-
-    def vcopy(out, in_, rd, wr):
-        op("V", lambda: g.vector.tensor_copy(out, in_), rd, wr)
-
-    def wrap(bank, col, src, skeys, z, c0, n, r0=0, r1=16):
-        for r in range(r0, r1):
-            mm(T[bank][:, col:col + n], T[z][:, 15 - r:143 - r], src[:, 16 * c0 + r:16 * (c0 + n):16],
-               r == 0, r == 15, skeys + [z], [bank])
-
-    def quarters(name):
-        return ["%s%d%s" % (name, q, h) for q in range(4) for h in "ab"]
-
-    for t in range(RO):
-        arrives("lr%d" % t, "ar%d" % t, from_(-HOPS[t]))
-        if t > 0:
-            arrives("xs%d" % t, "ax%d" % t, from_(-sum(HOPS[:t])))
-            arrives("ir%d" % t, "ai%d" % t, from_(-HOPS[t - 1]))
-    arrives("yla", "aa", from_(sum(HOPS)))
-    arrives("ylb", "ab", from_(sum(HOPS)))
-
-    dmas("ldo", [("Y", T.oi[:], T.o[:], [], ["oi"])])
-    dmas("ldx", [("S", T.xs[:, 0:4096], T.x[:], [], ["xs0"])])
-    iota(T.pi[:, 0:1], [[0, 1]], 0, 1, "pi", False)
-    iota(T.ramp[:], [[1, 64]], 0, 0, "ramp")
-    memset(T.idn[:], 0.0, "idn")
-    memset(T.dm[:, 1536:2048], 0.0, "dm3")
-    op("V", lambda: g.vector.tensor_scalar(T.pi[:, 1:2], T.pi[:, 0:1], 8, None, A.bitwise_and), ["pi"], ["pi8"])
-    memset(T.pm[:], 0.0, "pm")
-    vcopy(T.pf[:, 1:2], T.pi[:, 1:2], ["pi8"], ["pf1"])
-    memset(T.zo[:], 0.0, "zo")
-    op("V", lambda: g.vector.tensor_scalar(T.pf[:, 0:1], T.pf[:, 1:2], -1.0, 8.0, A.mult, A.add), ["pf1"], ["pf0"])
-    op("V", lambda: g.vector.tensor_scalar(T.tab[:, 0:64], T.ramp[:], T.pf[:, 1:2], 0.125, A.mult, A.mult), ["ramp", "pf1"], ["tab"])
-    op("V", lambda: g.vector.tensor_scalar(T.hc[:], T.ramp[:], T.pf[:, 0:1], 8.0, A.mult, A.mult), ["ramp", "pf0"], ["hc"])
-    for k in range(3):
-        n = 64 << k
-        op("V", lambda: g.vector.tensor_scalar(T.tab[:, n:2 * n], T.tab[:, 0:n], T.hc[:, n // 64:n // 64 + 1], None, A.add),
-           ["tab", "hc"], ["tab"])
-    for k in range(3):
-        n = 512 << k
-        op("S", lambda: g.scalar.activation(T.tab[:, n:2 * n], T.tab[:, 0:n], AF.Identity, bias=T.hc[:, n // 64:n // 64 + 1]),
-           ["tab", "hc"] + TABK[1:k + 1], [TABK[k + 1]])
-    op("S", lambda: g.scalar.activation(T.ft[:, 3584:4096], T.tab[:, 0:512], AF.Identity, bias=T.hc[:, 56:57]), ["tab", "hc"], ["ft3"])
-    vcopy(T.lo[:, 0:256], T.oi[:], ["oi"], ["loa0", "lob0", "loc0"])
-    sel(T.idn[:], [[-1, 128]], A.not_equal, 1.0, 0, 1, "idn")
-    d3 = T.dm[64:128, 1536:2048]
-    deps("G", ["idn"], [])
-    sel(d3, [[-1, 8], [-1, 8], [-8, 8]], A.not_equal, -1.0, 0, 1, "dm3")
-    sel(d3, [[-1, 8], [-1, 8], [-8, 8]], A.not_equal, -1.0, 8, 1, "dm3")
-    sel(d3, [[0, 64], [-8, 8]], A.is_ge, 0.0, 0, 1, "dm3")
-    sel(d3, [[0, 64], [8, 8]], A.is_ge, 0.0, 7, -1, "dm3")
-    sel(T.dm[0:64, 1536:2048], [[-1, 8], [0, 8], [-8, 8]], A.not_equal, 1.0, 0, 1, "dm3")
-
-    def perm(t):
-        sel(T.pm[:, 128 * t:128 * t + 128], [[-8 * 2 ** t, 8 // 2 ** t], [-64, 2], [-1, 8 * 2 ** t]],
-            A.not_equal, 1.0, 0, 1, "pm")
-
-    def round_consts(t):
-        c = 64 * t
-        side = [0] * 6
-        if t > 0:
-            side[t - 1] = 1
-        u = 32 if t == 0 else 1
-        for a, n, off, pat in pieces([-2 * s for s in side]):
-            iota(T.mk[:, c + a:c + a + n], pat, u + off, 0, "mk%d" % t)
-        for a, n, off, pat in pieces([-8 * w for w in CODE_W[t]] + [0]):
-            sel(T.mk[:, c + a:c + a + n], pat, A.is_ge, 0.0, off, 1, "mk%d" % t)
-        for a, n, off, pat in pieces([8 * w for w in CODE_W[t]] + [0]):
-            sel(T.mk[:, c + a:c + a + n], pat, A.is_ge, 0.0, 7 + off, -1, "mk%d" % t)
-        for a, n, off, pat in pieces(side[:5] + [-u]):
-            iota(T.cj[:, c + a:c + a + n], pat, off, u, "cj%d" % t)
-        w = [((16 if t else 1) << b) * (1 - 2 * side[b]) for b in range(5)] + [0]
-        for a, n, off, pat in pieces(w):
-            iota(T.bs[:, c + a:c + a + n], pat, off + sum((16 << b) * side[b] for b in range(5)), 0, "bs%d" % t)
-
-    perm(0)
-    mm(T.pw[:, 0:512], T.pm[:, 0:128], T.dm[:, 1536:2048], True, True, ["pm", "dm3"], ["pw"])
-    send(-1, T.lr[:, 0:256], T.lo[:, 0:256], "ar0", ["loa0"])
-    for name, n, v in (("zi", 144, 0), ("rm", 64, 0), ("lht", 256, 1), ("one", 32, 1)):
-        iota(T[name][:], [[0, n]], v, 0, name)
-    for z, o in (("zo", 0), ("zi", 4)):
-        sel(T[z][:, 15:128:16], [[16, 8]], A.not_equal, 1.0, o, -1, z)
-        sel(T[z][:, 15:128:16], [[16, 8]], A.not_equal, 1.0, o + 8, -1, z)
-    perm(1)
-    perm(2)
-    for q0 in range(2):
-        sel(T.lht[:, 128 * q0:128 * q0 + 128], [[0, 16], [-16, 8]], A.is_ge, 0.0, -8 * q0, 1, "lht")
-        sel(T.lht[:, 128 * q0:128 * q0 + 128], [[0, 16], [16, 8]], A.is_ge, 0.0, 8 * q0 + 7, -1, "lht")
-    sel(T.rm[:], [[-1, 8], [-8, 8]], A.not_equal, 8.0, 0, 1, "rm")
-    sel(T.rm[:], [[-1, 8], [-8, 8]], A.not_equal, 8.0, -64, 1, "rm")
-    iota(T.srow[:], [[0, 2], [1, 8]], 0, 0, "srow")
-    round_consts(0)
+    def memset(ap, v, keys):
+        op("V", lambda: g.vector.memset(ap, v), [], keys)
 
     def copy(e, out, in_, rd, wr):
         if e == "V":
-            vcopy(out, in_, rd, wr)
+            op(e, lambda: g.vector.tensor_copy(out, in_), rd, wr)
         else:
             op(e, lambda: g.scalar.activation(out, in_, AF.Copy), rd, wr)
 
-    def late_const(e, k):
-        if k == 0:
-            copy(e, T.dm[:, 0:512], T.pw[:, 0:512], ["pw"], ["dm0"])
-        elif k < 3:
-            bank = "d%d" % (k + 1)
-            mm(T[bank][:, 0:512], T.pm[:, 128 * k:128 * k + 128], T.dm[:, 1536:2048], True, True, ["pm", "dm3"], [bank])
-            copy(e, T.dm[:, 512 * k:512 * k + 512], T[bank][:, 0:512], [bank], ["dm%d" % k])
+    def ts(out, in0, s1, s2, ops, rd, wr):
+        op("V", lambda: g.vector.tensor_scalar(out, in0, s1, s2, *ops), rd, wr)
+
+    def keys(name, a, b):
+        return ["%s%d" % (name, k) for k in range(a, b)]
+
+    ZO, ZF, Z16, ZW, ZI = 0, 1, 2, 3, (4, 4, 5, 6, 6, 5)
+
+    def zeros(bank, col, n, start):
+        mm(T[bank][:, col:col + n], T.zz[0:1, 144:272], T.zz[0:1, 144:144 + n], start, not start, ["zz0", "zz1", "zz2"], [bank])
+
+    def fold(bank, col, src, name, z, so, cols, part, fixed, rows=128, mixed=False, only=None):
+        ws, wc, wp = wt(so), wt(cols), wt(part)
+        best = []
+        for i in range(len(cols)):
+            for k in range(i + 1, len(cols) + 1):
+                p = so.index(cols[i])
+                if so[p:p + k - i] == cols[i:k] and len(best) < k - i <= (6 if only is not None else 8):
+                    best = cols[i:k]
+        n = 1 << len(best)
+        rest = [b for b in cols if b not in best]
+        calls = []
+        for vc in values(rest):
+            for vp in values(part):
+                calls.append((dot(ws, vc) + dot(ws, vp) + dot(ws, fixed), dot(wc, vc), dot(wp, vp)))
+        if mixed:
+            calls.sort()
+            zeros(bank, col, 1 << len(cols), True)
+        for i, (s0, c0, r) in enumerate(calls):
+            if only is not None and i // 16 != only:
+                continue
+            ss, cs = ws[best[-1]], wc[best[-1]]
+            last = s0 + ss * (n - 1)
+            a = 144 * z + 15 - r
+            mm(T[bank][:, col + c0:col + c0 + cs * (n - 1) + 1:cs], T.zz[0:rows, a:a + 128], src[0:rows, s0:last + 1:ss],
+               not mixed and i % 16 == 0, not mixed and i % 16 == 15,
+               keys(name, s0 // 256, last // 256 + 1) + ["zz%d" % z], [bank])
+        if mixed:
+            zeros(bank, col, 1 << len(cols), False)
+
+    def plain(bank, col, name, z, half):
+        fold(bank, col, T[name], name, z, NATURAL, NATURAL[1:8], NATURAL[8:], {"y2": half})
+
+    for t in range(RO):
+        arrives("lr%d" % t, "ar%d" % t, width(peer(HOPS[t]), core))
+        arrives("kr%d" % t, "ak%d" % t, width(partner, core))
+        for s in range(ND[t]):
+            arrives("mp%d_%d" % (t, s), "af%d_%d" % (t, s), width(partner, core))
+        if t > 0:
+            arrives("xs%d" % t, "ax%d" % t, width(peer(sum(HOPS[:t])), core))
+            arrives("ir%d" % t, "ai%d" % t, width(peer(HOPS[t - 1]), core))
+    arrives("yl", "ay", width(peer(-sum(HOPS)), core))
+
+    dmas("ldo", [("Y", T.oi[:], T.o[:], [], ["oi"])])
+    dmas("ldx", [("Y", T.xs[:, 0:4096], T.x[:], [], ["xs0"])])
+    iota(T.pi[:, 0:4], [[-4, 4]], 16, 1, "pi", False)
+    iota(T.ramp[:], [[1, 8]], 0, 0, "ramp")
+    memset(T.idn[:], 0.0, ["idn"])
+    ts(T.pi[:, 4:8], T.pi[:, 0:4], 15, None, [A.bitwise_and], ["pi"], ["pj"])
+    memset(T.dm[:, 512:1024], 0.0, ["dm1"])
+    ts(T.mk[:], T.pi[:, 4:8], 0.0, None, [A.is_equal], ["pj"], ["mk"])
+    memset(T.pm[:], 0.0, ["pm"])
+    ts(T.tab[:, 0:8], T.ramp[:], T.mk[:, 0:1], None, [A.mult], ["ramp", "mk"], ["tab0"])
+    ts(T.hc[:], T.ramp[:], T.mk[:, 0:1], 8.0, [A.mult, A.mult], ["ramp", "mk"], ["hc"])
+    for k in range(6):
+        n = 8 << k
+        f = [i for i in range(3) if "b%d" % k in FIELDS[i]][0]
+        m = T.mk[:, f + 1:f + 2]
+        key = "tab1" if k == 5 else "tab0"
+        if FIELDS[f][0] == "b%d" % k:
+            ts(T.tab[:, n:2 * n], T.tab[:, 0:n], m, m, [A.add, A.add], ["tab0", "mk"], [key])
         else:
-            for q0 in range(2):
-                mm(T.pw[:, 128 * q0:128 * q0 + 128], T.lht[:, 128 * q0:128 * q0 + 128], T.idn[:], True, True,
-                   ["lht", "idn"], ["pw"])
-            copy(e, T.lh[:], T.pw[:, 0:256], ["pw"], ["lh"])
+            ts(T.tab[:, n:2 * n], T.tab[:, 0:n], m, None, [A.add], ["tab0", "mk"], [key])
+    for k in range(3):
+        n = 512 << k
+        op("S", lambda: g.scalar.activation(T.tab[:, n:2 * n], T.tab[:, 0:n], AF.Identity, bias=T.hc[:, 1 << k:(1 << k) + 1]),
+           keys("tab", 0, n // 256) + ["hc"], keys("tab", n // 256, n // 128))
+    memset(T.zz[:, 0:432], 0.0, ["zz0", "zz1", "zz2"])
+    ts(T.hl[:, 0:256], T.oi[:], BIG64, -BIG64, [A.add, A.add], ["oi"], ["hl0"])
+    memset(T.zz[:, 432:1008], 0.0, ["zz3", "zz4", "zz5", "zz6"])
+    op("V", lambda: g.vector.tensor_tensor(T.hl[:, 256:512], T.oi[:], T.hl[:, 0:256], A.subtract), ["oi", "hl0"], ["hl1"])
+    dmas("fst", [("Y", T.fo[k:16:2, 2048 * h:2048 * h + 2048], T.hl[:, 256 * k + 128 * h:256 * k + 128 * h + 128],
+                  ["hl%d" % k], keys("fo", 8 * h, 8 * h + 8)) for k in range(2) for h in range(2)])
+    dmas("late", [("Y", T.inv1[:, 512 * LATE:4096], T.tab[:, 512 * LATE:4096], keys("tab", 2 * LATE, 16), keys("inv1", 2 * LATE, 16))])
+    copy("V", T.ln[:], T.oi[:], ["oi"], ["ln"])
+    memset(T.cf[:], 0.0, ["z0", "z1", "rm", "pq0", "pq1"])
 
-    def window_dmas(dst, col, key, gs):
-        dmas("owd", [("Y", dst[16 * y:16 * y + 16, col:col + 512], T.fo[0:128:8, 512 * y:512 * y + 512],
-                      ["fo%da" % (y // 2), "fo%db" % (y // 2)], [key]) for y in gs])
+    sel(T.idn[:], [[-1, 128]], 1.0, 0, "idn")
+    for fill, step, base in ((1.0, 0, 0), (-1.0, -16, -1), (-1.0, -16, 127)):
+        sel(T.dm[:, 512:1024], [[-16, 8], [-2, 8], [step, 8]], fill, base, "dm1")
+    side, q, a, c, r4 = roles(0)
+    w = wt(J + a + [q, side])
+    for c0, n, off, pat in pieces([-w[b] for b in reversed(NATURAL[5:])]):
+        sel(T.pm[:, c0:c0 + n], pat, 1.0, off, "pm")
+    for k in range(2):
+        sel(T.zz[:, 144 * Z16 + 15:144 * Z16 + 128:16], [[-2, 8]], 1.0, -k, "zz%d" % Z16)
 
-    later = {}
+    def selector(z, rows):
+        for row, weight in rows:
+            sel(T.zz[:, 144 * z + 15:144 * z + 128:16], [[-16, 8]], float(weight), -row, "zz%d" % z)
 
-    def scatter(q):
-        src, key = (T.ft, "ft3") if q == 7 else (T.tab, TABK[q.bit_length()])
-        op("V", lambda: g.vector.tensor_copy(T.inv0[:, 0:4096].indirect(T.lo[:, 32 * q:32 * q + 32]),
-                                             src[:, 512 * q:512 * q + 512]), [key, "lob0"], quarters("inv0"))
+    def inverse_selector(t):
+        selector(ZI[t], [(0, 64)] + [(4 + 4 * f, v) for f, v in zip(ROLES[t], (16, 4, 1))])
 
-    def scores(t):
-        vs, ss = (V_SEQ0, S_SEQ0) if t == 0 else (V_SEQ, S_SEQ)
-        c0 = 256 * t
-        dk = min(t, 3)
-        steps = []
-        ready = {}
-        clock = {"V": 0.0, "S": 0.0}
-        pos = {"V": 0, "S": 0}
-        seq = {"V": vs, "S": ss}
-        used = [0] * 4
-        nb = {"V": 0, "S": 0}
-        free = {}
-        while pos["V"] < len(vs) or pos["S"] < len(ss):
-            cand = []
-            for e in "VS":
-                if pos[e] < len(seq[e]):
-                    s = seq[e][pos[e]]
-                    q = s[-1]
-                    need = {"e": ["ga" + q, "gb" + q], "r": ["e" + q] + (["c0"] if t == 0 else []),
-                            "i": ["o2"], "g": ["o1"] if t and chunk(CUTS, int(q)) else []}.get(s[0], [])
-                    if all(k in ready for k in need):
-                        cand.append((max([clock[e]] + [ready[k] + 0.6 for k in need]), e, s, need))
-            at, e, s, need = min(cand)
-            if s[0] == "e":
-                tt = max([ready[k] for k in need] + [ready.get("e%d" % (int(s[1]) - 2), 0.0)])
-                steps.append((tt, 0, "P", "t", int(s[1]), None))
-                at = max(at, tt)
-                steps.append((at, 1, e, s, None, None))
-            elif s[0] == "r":
-                n = 8 * int(s[1]) + used[int(s[1])]
-                used[int(s[1])] += 1
-                bank = "d%d" % ((0 if e == "V" else 2) + nb[e] % 2)
-                nb[e] += 1
-                steps.append((max([free.get(bank, 0.0)] + [ready[k] for k in need]), 0, "P", "d", n, bank))
-                steps.append((at, 1, e, "r", n, bank))
-                free[bank] = at + COST["r"]
-            else:
-                steps.append((at, 1, e, s, None, None))
-            clock[e] = at + COST[s[0]] * (int(s[2]) - int(s[1]) if s[0] == "i" else 1)
-            ready[s] = clock[e]
-            pos[e] += 1
-        assert used == [8] * 4
-        order = sorted(range(len(steps)), key=lambda i: (steps[i][0] - (0.0 if steps[i][1] else 1e-6 * 0), i))
-        for i in order:
-            at, _, e, s, n, bank = steps[i]
-            if s[0] == "g":
-                q, hf = int(s[2]), "ab".index(s[1])
-                a = 64 * q + 32 * hf
-                gather(e, T.xo[:, 16 * a:16 * a + 512], T.xs[:, 4096 * t:4096 * t + 4096], T.lo[:, c0 + a:c0 + a + 32],
-                       ["xs%d" % t, "lo%s%d" % ("abc"[chunk(CUTS, q)], t)], ["xo%d%s" % (q, s[1])])
-            elif s == "t":
-                tb = "t%d" % (n % 2)
-                for b in range(8):
-                    y, b2 = 2 * n + b // 4, b % 4
-                    rd = ["xo%d%s" % (n, "ab"[b // 4]), "idn"]
-                    if t <= 3:
-                        parts = [(0, 128, 512 * y + 128 * b2)]
-                    elif t == 4:
-                        a = 512 * y + 256 * (b2 >> 1) + 64 * (b2 & 1)
-                        parts = [(0, 64, a), (64, 64, a + 128)]
-                    else:
-                        a = 512 * y + 64 * b2
-                        parts = [(0, 64, a), (64, 64, a + 256)]
-                    for p, m, a in parts:
-                        op("P", lambda: g.tensor.transpose(T[tb][p:p + m, 128 * b:128 * b + 128], T.xo[:, a:a + m], T.idn[:]),
-                           rd, [tb])
-            elif s[0] == "e":
-                q = int(s[1])
-                vcopy(T.xt[:, 1024 * q:1024 * q + 1024], T["t%d" % (q % 2)][:, 0:1024], ["t%d" % (q % 2)], ["xt%d" % q])
-            elif s == "d":
-                for ml in range(4):
-                    a = 512 * dk + 128 * ml
-                    mm(T[bank][:, 128 * ml:128 * ml + 128], T.dm[:, a:a + 128], T.xt[:, 128 * n:128 * n + 128], True, True,
-                       ["dm%d" % dk, "xt%d" % (n // 8)], [bank])
-            elif s == "r":
-                col = 8 * (n % 4) + n // 4
-                if e == "V":
-                    op(e, lambda: g.vector.tensor_reduce(T.sc[:, col:col + 1], T[bank][:, 0:512], AxisListType.X, A.add,
-                                                         apply_absolute_value=True), [bank], ["sc%d" % col])
-                else:
-                    j = 512 * (n % 8)
-                    op(e, lambda: g.scalar.activation(T.junk[:, j:j + 512], T[bank][:, 0:512], AF.Abs,
-                                                      accum_out=T.sc[:, col:col + 1]), [bank], ["sc%d" % col, "junk%d" % (n % 8)])
-            elif s[0] == "s":
-                scatter(int(s[1]))
-            elif s[0] == "u":
-                op(e, lambda: g.vector.tensor_scalar(T.hl[:, 0:256], T.oi[:], BIG64, -BIG64, A.add, A.add), ["oi"], ["hl0"])
-                op(e, lambda: g.vector.tensor_tensor(T.hl[:, 256:512], T.oi[:], T.hl[:, 0:256], A.subtract), ["oi", "hl0"], ["hl1"])
-                op(e, lambda: g.vector.tensor_scalar(T.pf[:, 2:3], T.pf[:, 0:1], 32.0, None, A.mult), ["pf0"], ["pf2"])
-                dmas("owd", [("Y", T.ow[16 * y + k:16 * y + 16:2, 0:512], T.hl[:, 256 * k + 32 * y:256 * k + 32 * y + 32],
-                              ["hl%d" % k, "xs0"], ["ow0"]) for k in range(2) for y in range(8)])
-            elif s[0] == "o":
-                later[s]()
-                if s == "o1":
-                    later["rest"]()
-            elif s[0] == "i":
-                inv_part(e, t, int(s[1]), int(s[2]))
-            else:
-                late_const(e, int(s[1]))
+    def movers(t):
+        side, q, a, c, r4 = roles(t)
+        w = wt(FIRST[5:] if t == 0 else a + [q] + Y[1:] + c)
+        for v in range(2):
+            for c0, n, off, pat in pieces([-w[b] for b in reversed(Y[1:] + r4)]):
+                p = 320 + 128 * t + 64 * v + c0
+                sel(T.cf[:, p:p + n], pat, -512.0, off - w[q] * v, "pq%d" % t)
+
+    def window_consts():
+        sel(T.zz[:, 144 * ZW:144 * ZW + 48], [[-1, 48]], 1.0, 16, "zz%d" % ZW)
+        iota(T.one[:], [[0, 128]], 1, 0, "one")
+
+    def key_consts():
+        iota(T.srow[:, 0:16], [[0, 2], [64, 8]], 0, 0, "srow")
+        iota(T.srow[:, 16:32], [[0, 16]], 0, 0, "srow")
+        for h in range(2):
+            sel(T.cf[:, 192:320], [[-16, 4], [0, 2], [-1, 16]], 512.0, -64 * h, "rm")
+
+    def list_consts():
+        inverse_selector(0)
+        selector(ZF, [(4, 1), (12, 1)])
+        selector(ZO, [(0, 1), (8, 1)])
+
+    def offset_consts(t):
+        side, q, a, c, r4 = roles(t)
+        w = wt(STAR[6:] if t == 0 else order(0)[6:])
+        if t == 0:
+            iota(T.row[:, 384:512], [[0, 128]], 1, 0, "row")
+            iota(T.row[:, 0:128], [[0, 8], [w[r4[1]], 4], [0, 4]], 0, 0, "row")
+            iota(T.row[:, 128:256], [[0, 32], [w[r4[2]], 2], [w[r4[3]], 2]], 0, 0, "row")
+        else:
+            iota(T.row[:, 256:384], [[0, 8], [w[r4[1]], 4], [w[r4[3]], 4]], 0, 0, "row")
+        for sd in range(2):
+            for back in range(2):
+                js = [(j - back) % 8 if sd == 0 else (j + 1 - back) % 8 + 8 for j in range(8)]
+                j0 = 0
+                for j in range(1, 9):
+                    if j == 8 or js[j] != js[j - 1] + 1:
+                        p = 64 * t + 32 * sd + 16 * back + 2 * j0
+                        iota(T.base[:, p:p + 2 * (j - j0)], [[64, j - j0], [w[q], 2]], 64 * js[j0] + w[side] * (1 - sd), 0,
+                             "base%d" % t)
+                        j0 = j
+
+    def offsets(t, bank):
+        out = T[bank][:, 0:64]
+        mm(out, T.row[0:1, 384:512], T.base[0:1, 64 * t:64 * t + 64], True, False, ["row", "base%d" % t], [bank])
+        for k in ((0, 1), (2,))[t]:
+            mm(out, T.row[0:1, 128 * k:128 * k + 128], T.row[0:1, 384:448], False, k > 0, ["row"], [bank])
+
+    def first_window(part):
+        ws, ww = wt(FIRST), wt(STAR[3:])
+        for v in values(["b0"] + J)[2 * part:2 * part + 2]:
+            for y in values(Y):
+                p, s0, c0 = 32 * (2 * y["y2"] + y["y1"]), dot(ws, v) + dot(ws, y), dot(ww, v)
+                z = 144 * ZW + 16 - 16 * y["y0"]
+                mm(T.pa[p:p + 32, c0:c0 + 32], T.zz[0:16, z:z + 32], T.fo[0:16, s0:s0 + 32], y["y0"] == 0, y["y0"] == 1,
+                   keys("fo", 0, 16) + ["zz%d" % ZW], ["pa"])
+
+    def send_x(t):
+        send(peer(-sum(HOPS[:t])), T.xs[:, 4096 * t:4096 * t + 4096], T.xs[:, 0:4096], "ax%d" % t, ["xs0"])
+
+    consts = [lambda: send_x(1), window_consts, key_consts, lambda: movers(0), lambda: offset_consts(0), list_consts]
 
     def inv_part(e, t, a, b):
         old, new = "inv%d" % ((t - 1) % 2), "inv%d" % (t % 2)
-        gather(e, T[new][:, 512 * a:512 * b], T[old][:, 0:4096], T.lf[:, 256 * t + 32 * a:256 * t + 32 * b],
-               quarters(old) + ["lf%d" % t], quarters(new)[a:b])
+        gather(e, T[new][:, 256 * a:256 * b], T[old][:, 0:4096], T.lf[:, 16 * a:16 * b], keys(old, 0, 16) + ["lf"], keys(new, a, b))
 
-    def inv_wrap(t, q):
-        name = "inv%d" % (t % 2)
-        wrap(("pw", "d0")[q // 2], 64 * (q % 2), T[name], quarters(name)[2 * q:2 * q + 2], "zo", 64 * q, 64)
+    def scatter(q):
+        src = "inv1" if q >= LATE else "tab"
+        op("V", lambda: g.vector.tensor_copy(T.inv0[:, 0:4096].indirect(T.ln[:, 32 * q:32 * q + 32]), T[src][:, 512 * q:512 * q + 512]),
+           keys(src, 2 * q, 2 * q + 2) + ["ln"], keys("inv0", 0, 16))
+
+    def lower_list(t):
+        side, q, a, c, r4 = roles(t)
+        if t == 0:
+            fold("d2", 0, T.fo, "fo", Z16, FIRST, FIRST[1:8], FIRST[8:], {"y2": 0}, rows=16)
+        else:
+            fold("d2", 0, T.fo, "fo", ZO, order(t - 1), [side] + J + a + [q], Y[1:] + c, {"y2": 0}, mixed=True)
+
+    def scores(t):
+        side, q, a, c, r4 = roles(t)
+        w4 = wt(r4)
+        nd, m0 = ND[t], sum(ND[:t])
+        dk = min(t, 1)
+        zc = 96 * dk
+        pad = w4[a[0]] + w4[a[1]]
+        seq = {e: v.split() for e, v in (SEQ0 if t == 0 else SEQ).items()}
+        every = seq["V"] + seq["S"]
+
+        def span(s):
+            return [int(v) for v in s[1:].split(":")]
+
+        def covering(kind, k):
+            return [s for s in every if s[0] == kind and span(s)[0] <= k < span(s)[1]]
+
+        def gathered(a0, b0):
+            return [s for k in range(a0, b0) for s in covering("g", k)]
+
+        def sums(col, src, p, key):
+            for j in range(8):
+                mm(T.pl[:, col:col + 1], src[:, p + 128 * j:p + 128 * j + 128], T.one[:, 0:1], j == 0, j == 7, [key, "one"], ["pl"])
+
+        def move(src, a0, b0, key, v):
+            for k in (v, 2 + v):
+                p = 320 + 128 * dk + 64 * v
+                mm(T.pk[0:64, 8 * k + a0:8 * k + b0], T.cf[:, p:p + 64], src, False, False, [key, "pq%d" % dk], ["pk"])
+
+        def turn(k):
+            for b in range(4):
+                p = H1 + 512 * k
+                in_ = T.xo[:, p + 128 * b:p + 128 * b + 128] if t == 0 else T.xo[:, p + b:p + 512:4]
+                o = 512 * (k % 2) + 128 * b
+                op("P", lambda: g.tensor.transpose(T.tb[:, o:o + 128], in_, T.idn[:]), keys("xo", 8 + 2 * k, 10 + 2 * k) + ["idn"], ["tb"])
+
+        def differences(k):
+            bank = "d%d" % (k % 3)
+            for m in range(4):
+                p = 512 * dk + 128 * m
+                mm(T[bank][:, 128 * m:128 * m + 128], T.dm[:, p:p + 128], T.xt[:, 128 * k:128 * k + 128], True, True,
+                   ["dm%d" % dk, "xt%d" % (k // 4)], [bank])
+
+        def side_zero(h):
+            mm(T.pa[:, 512 * h:512 * h + 512], T.idn[:], T.xo[:, 512 * h:512 * h + 512], True, True,
+               keys("xo", 2 * h, 2 * h + 2) + ["idn"], ["pa"])
+
+        def upper_keys(h):
+            if h == 0:
+                mm(T.pk[:, 0:32], T.one[0:1, 0:128], T.srow[0:1, 0:32], True, False, ["one", "srow"], ["pk"])
+            for k in range(4):
+                p = zc + 48 * h + pad - w4[a[0]] * (k // 2) - w4[a[1]] * (k % 2)
+                mm(T.pk[64 + 32 * h:96 + 32 * h, 0:32], T.cf[:, p:p + 32], T.cf[:, 192 + 32 * k:224 + 32 * k], False,
+                   False, ["rm"] + keys("sc", 8 * h, 8 * h + 8), ["pk"])
+            if h == 1:
+                zeros("pk", 0, 32, False)
+
+        def out_list(k):
+            o = order(t)
+            if t == 0:
+                fold("pl", 256, T.fo, "fo", Z16, STAR, o[:8], o[8:], {}, rows=16, only=k)
+            else:
+                fold("pl", 256, T.fo, "fo", ZO, order(t - 1), o[:8], o[8:], {}, only=k)
+
+        pe = {}
+        if t == 0:
+            pe["x"] = (0.95, [], lambda: lower_list(0))
+            pe["C0"] = (0.25, [], lambda: mm(T.pk[:, 0:512], T.pm[:], T.dm[:, 512:1024], True, True, ["pm", "dm1"], ["pk"]))
+        else:
+            pe["x"] = (0.5, [], lambda: None)
+        for k in range(16):
+            pe["d%d" % k] = (0.24, covering("e", k // 4) + (["r%d" % (k - 3)] if k > 2 else ["x0"]) + (["c0"] if t == 0 else []),
+                             lambda k=k: differences(k))
+        for k in range(4):
+            pe["t%d" % k] = (0.24, gathered(8 + 2 * k, 10 + 2 * k) + (covering("e", k - 2) if k > 1 else []), lambda k=k: turn(k))
+        for k in range(8 if t == 0 else 0):
+            pe["W%d" % k] = (0.25, ["G1", "x0"], lambda k=k: first_window(k))
+        for h in range(2):
+            pe["a%d" % h] = (0.24, gathered(2 * h, 2 * h + 2) + (["o"] if t == 0 else []), lambda h=h: side_zero(h))
+        for k in range(nd):
+            pe["p%d" % k] = (0.25, ["A%d" % k], lambda k=k: sums(8 + k, T.mp, 1024 * (m0 + k), "mp%d_%d" % (t, k)))
+        for k in range(nd, 8):
+            pe["n%d" % k] = (0.25, ["m%d" % k], lambda k=k: sums(k, T.ml, 1024 * k, "ml%d" % k))
+        if t == 0:
+            pe["CB"] = (0.3, ["G4", "c0"], lambda: offsets(0, "pk"))
+        for k in range(4):
+            pe["w%d" % k] = (0.5, ["O"] if t == 0 else ["a0", "a1", "d%d" % (3 + 2 * k)], lambda k=k: out_list(k))
+        pe["k0"] = (0.3, ["r7"] + (["G2", "cb"] if t == 0 else ["lf"]), lambda: upper_keys(0))
+        for v in range(2):
+            pe["kL%d" % v] = (0.25, ["kl", "k0"], lambda v=v: move(T.kl[:, nd:8], nd, 8, "kl", v))
+            pe["kR%d" % v] = (0.25, ["R", "k0"], lambda v=v: move(T.kr[:, 8 * t:8 * t + nd], 0, nd, "kr%d" % t, v))
+        pe["k1"] = (0.25, ["r15", "kL0", "kL1", "kR0", "kR1"], lambda: upper_keys(1))
+
+        def needs(s):
+            if s[0] == "g":
+                return ["x0"] if span(s)[0] < 8 else []
+            if s[0] == "e":
+                return ["t%d" % k for k in range(*span(s))]
+            if s[0] == "f":
+                return gathered(0, 8) + (["u"] if s != "f0" else [])
+            if s[0] in "rm":
+                return ["d" + s[1:]] if s[0] == "r" else ["a0", "a1"] + gathered(4, 8)
+            return {"u": gathered(4, 8), "x0": ["x"], "c0": ["C0"], "cb": ["CB"], "o": ["W%d" % k for k in range(8)], "K": ["kp"],
+                    "kp": ["p%d" % k for k in range(nd)], "kl": ["n%d" % k for k in range(nd, 8)]}.get(s, ["lf"] if s[0] == "i" else [])
+
+        def call(e, s):
+            n = span(s) if s[1:2].isdigit() else []
+            if s[0] == "g":
+                p = 256 * n[0] + (DUP if n[0] >= 8 else 0)
+                lst, key = (T.ln, "ln") if t == 0 and n[0] >= 8 else (T.lx, "lx%d" % (n[0] // 8))
+                gather(e, T.xo[:, p:p + 256 * (n[1] - n[0])], T.xs[:, 4096 * t:4096 * t + 4096], lst[:, 16 * n[0]:16 * n[1]],
+                       ["xs%d" % t, key], keys("xo", n[0], n[1]))
+            elif s == "u":
+                copy(e, T.xo[:, 2048:2048 + 128 * (nd - 1)], T.xo[:, 1024:1024 + 128 * (nd - 1)], keys("xo", 4, 8), ["dup"])
+            elif s[0] == "f":
+                rd = keys("xo", 0, 8) + (["dup"] if n[0] else [])
+                deps("G", rd, ())
+                rid, pid, _ = topo.addr(partner)
+                p, b = 1024 * (m0 + n[0]), 1024 + 128 * n[0]
+                g.remote_dma_fused([RemoteDMATransfer(
+                    dst_ids=[DstId(rid=rid, pnc=pid)], dma_engine_mask=topo.mask(core, partner),
+                    remote_sem=T.sem["af%d_%d" % (t, n[0])], srcs=[T.xo[:, 0:1024], T.xo[:, b:b + 1024]],
+                    dsts=[T.mp[:, p:p + 1024]], alu_op=3)], local_sem=T.sem.sf)
+                count["sf"] = count.get("sf", 0) + width(core, partner)
+                for k in rd:
+                    readers[k] = [tok for tok in readers.get(k, []) if tok[0] != "sf"] + [("sf", count["sf"])]
+            elif s == "x0":
+                copy(e, T.lx[:, 0:128], T.d2[:, 0:128], ["d2"], ["lx0"])
+            elif s[0] == "e":
+                o = 512 * (n[0] % 2)
+                copy(e, T.xt[:, 512 * n[0]:512 * n[1]], T.tb[:, o:o + 512 * (n[1] - n[0])], ["tb"], keys("xt", n[0], n[1]))
+            elif s[0] == "r":
+                k = n[0]
+                hi, lo = (c[1], c[0]) if t == 0 else c
+                col = zc + 48 * (k // 8) + pad + 16 * (k // 4 % 2) + w4[hi] * (k // 2 % 2) + w4[lo] * (k % 2)
+                j, bank = 512 * (k % 2), "d%d" % (k % 3)
+                op(e, lambda: g.scalar.activation(T.junk[:, j:j + 512], T[bank][:, 0:512], AF.Abs, accum_out=T.cf[:, col:col + 1]),
+                   [bank, "z%d" % dk], ["sc%d" % k, "junk%d" % (k % 2)])
+            elif s[0] == "m":
+                k = n[0]
+                deps(e, (), ["ml%d" % k])
+                for a0, b0, w in ((0, k, 8 - k), (8 - k, 0, k)):
+                    p = 1024 * k + 128 * a0
+                    op(e, lambda: g.vector.tensor_tensor(T.ml[:, p:p + 128 * w], T.xo[:, 1024 + 128 * b0:1024 + 128 * (b0 + w)],
+                                                         T.pa[:, 128 * a0:128 * (a0 + w)], A.min),
+                       keys("xo", 4, 8) + ["pa"], ["ml%d" % k] if a0 else [])
+            elif s == "kp":
+                copy(e, T.ks[:, 8 * t:8 * t + nd], T.pl[:, 8:8 + nd], ["pl"], ["ks%d" % t])
+            elif s == "K":
+                send(partner, T.kr[:, 8 * t:8 * t + nd], T.ks[:, 8 * t:8 * t + nd], "ak%d" % t, ["ks%d" % t])
+            elif s == "kl":
+                copy(e, T.kl[:, nd:8], T.pl[:, nd:8], ["pl"], ["kl"])
+            elif s[0] == "i":
+                inv_part(e, t, n[0], n[1])
+            elif s == "lf":
+                copy(e, T.lf[:], T.pk[:, 256:512], ["pk"], ["lf"])
+            elif s == "o":
+                for h in range(2):
+                    copy(e, T.ow[:, 512 * h:512 * h + 512], T.pa[:, 0:512], ["pa"], ["ow0%d" % h])
+                dmas("owd", [("Y", T.fo[0:16, 512 * y:512 * y + 512], T.ow[16 * y:16 * y + 16, 0:512], ["ow00"],
+                              keys("fo", 0, 16)) for y in range(8)])
+            elif s[0] == "s":
+                scatter(n[0])
+            elif s == "c0":
+                copy(e, T.dm[:, 0:512], T.pk[:, 0:512], ["pk"], ["dm0"])
+            elif s == "cb":
+                copy(e, T.base[:, 0:64], T.pk[:, 0:64], ["pk"], ["base0"])
+            else:
+                consts[n[0]]()
+
+        lands = {"K": "R", "o": "O"}
+        done, steps = {}, []
+        clock = dict(zip("VSGP", START if t == 0 else (0.0,) * 4))
+        left = list(pe)
+        while left or any(seq[e] for e in "VSG"):
+            cand = []
+            for e in "VSGP":
+                for s in (left if e == "P" else seq[e][:1]):
+                    need = pe[s][1] if e == "P" else needs(s)
+                    if all(k in done for k in need):
+                        cand.append((max([clock[e]] + [done[k] + 0.1 for k in need]), len(cand), e, s))
+            at, _, e, s = min(cand)
+            if e == "P":
+                left.remove(s)
+                clock[e] = at + pe[s][0]
+            else:
+                seq[e].pop(0)
+                clock[e] = at + COST[s[0]] * (span(s)[1] - span(s)[0] if ":" in s else 1)
+            done[s] = clock[e]
+            if s[0] == "f":
+                done["A" + s[1:]] = max(clock[e] + 1.0, done.get("A%d" % (int(s[1:]) - 1), 0.0)) + FOLD
+            if s in lands:
+                done[lands[s]] = clock[e] + HOP
+            steps.append((e, s))
+        for e, s in steps:
+            if e == "P":
+                pe[s][2]()
+            else:
+                call(e, s)
 
     def shifts(t):
-        c = 64 * t
+        side, q, a, c, r4 = roles(t)
+        last = t == RO - 1
+        name = "inv%d" % (t % 2)
+        dk = min(t, 1)
         if t > 0:
-            inv_part("S", t, INV_MID, INV_END)
-        else:
-            late_const("S", 1)
-            late_const("S", 2)
-        for a in range(4):
-            out = T.pk[32 * a:32 * a + 32, 0:16]
-            mm(out, T.one[0:1, 0:32], T.srow[0:1, 0:16], True, False, ["one", "srow"], ["pk"])
-            mm(out, T.sc[:, 0:32], T.rm[:, 16 * a:16 * a + 16], False, True, ["rm"] + ["sc%d" % k for k in range(32)], ["pk"])
-        for q0 in range(2):
-            op("V", lambda: g.vector.tensor_reduce(T.km[:, q0:q0 + 1], T.pk[:, 8 * q0:8 * q0 + 8], AxisListType.X, A.min),
-               ["pk"], ["km%d" % q0])
-        if t == 0:
-            for k in range(4):
-                q0, sd = k % 2, k // 2
-                op("V", lambda: g.vector.tensor_scalar(T.rh[:, 64 * sd + q0:64 * sd + 64:2], T.mk[:, q0:64:2], T.km[:, q0:q0 + 1],
-                                                       1.0 - 2 * sd, A.mult, A.mult), ["mk0", "km%d" % q0], ["rh%d" % k])
-            mm(T.pk[:, 64:128], T.lh[:, 128:256], T.mk[:, 0:64], True, False, ["lh", "mk0"], ["pk"])
-        else:
-            for q0 in range(2):
-                op("V", lambda: g.vector.tensor_scalar(T.rh[:, 64 * q0:64 * q0 + 64], T.mk[:, c:c + 64], T.km[:, q0:q0 + 1],
-                                                       None, A.mult), ["mk%d" % t, "km%d" % q0], ["rh%d" % q0, "rh%d" % (q0 + 2)])
-        for q0 in range(2):
-            mm(T.pk[:, 64:128], T.lh[:, 128 * q0:128 * q0 + 128], T.rh[:, 64 * q0:64 * q0 + 64], q0 == 0 and t > 0, q0 == 1,
-               ["lh", "rh0", "rh1", "rh2", "rh3"], ["pk"])
-        if t > 0:
-            inv_wrap(t, 0)
-        op("V", lambda: g.vector.tensor_tensor(T.i1[:], T.pk[:, 64:128], T.cj[:, c:c + 64], A.add), ["pk", "cj%d" % t], ["i1"])
-        op("V", lambda: g.vector.tensor_scalar(T.i2[:], T.i1[:], 7 if t else 224, None, A.bitwise_and), ["i1"], ["i2"])
-        op("V", lambda: g.vector.tensor_tensor(T.i3[:], T.i2[:], T.bs[:, c:c + 64], A.add), ["i2", "bs%d" % t], ["i3"])
-        pc = 1 if t else 2
-        op("V", lambda: g.vector.tensor_scalar(T.rl[:], T.i3[:], T.pf[:, pc:pc + 1], None, A.add), ["i3", "pf%d" % pc], ["rl"])
-        win = T.ow[:, 512 * t:512 * t + 512]
-        n = 1 if t == RO - 1 else 2
-        gather("V", T.bo[:, 0:256 * n], win, T.rl[:, 0:16 * n], ["rl", "ow%d" % t], ["boa"])
-        gather("S", T.bo[:, 256 * n:512 * n], win, T.rl[:, 16 * n:32 * n], ["rl", "ow%d" % t], ["bob"])
+            inv_part("S", t, INV_PRE, INV_MID)
+        for k in range(4):
+            op("V", lambda: g.vector.tensor_reduce(T.km[:, k:k + 1], T.pk[:, 8 * k:8 * k + 8], AxisListType.X, A.min),
+               ["pk"], ["km%d" % k])
+        n = 1 if last else 2
+        w = wt(FIELDS[ROLES[t][0]])
+        for sd in range(2):
+            for v in range(2):
+                p, o = 64 * dk + 32 * sd + v, w[side] * sd + w[q] * v
+                ts(T.rl[:, o:32 * n:4], T.base[:, p:p + 16 * n - 1:2], T.km[:, v:v + 1], T.km[:, 2 + v:3 + v],
+                   [A.subtract, A.add] if sd else [A.add, A.subtract], ["base%d" % dk, "km%d" % v, "km%d" % (2 + v)], ["rl%d" % o])
+        p = 1024 * (t % 2)
+        win = T.ow[:, p:p + 1024]
+        rd = keys("rl", 0, 4) + ["ow%d0" % (t % 2), "ow%d1" % (t % 2)]
+        gather("V", T.bo[:, 0:256 * n], win, T.rl[:, 0:16 * n], rd, ["boa"])
+        gather("S", T.bo[:, 256 * n:512 * n], win, T.rl[:, 16 * n:32 * n], rd, ["bob"])
         dmas("tabd", [("YS"[y % 2], T.tab[0:128:8 // n, 512 * y:512 * y + 512], T.bo[16 * y:16 * y + 16, 0:512 * n],
-                       ["boa", "bob"], TABK) for y in range(8)])
+                       ["boa", "bob"], keys("tab", 2 * y, 2 * y + 2)) for y in range(8)])
+        copy("V", T.ls[:, 256 * t:256 * t + 256], T.pl[:, 256:512], ["pl"], ["ls%d" % t])
+        send(peer(-HOPS[t]), T.lr[:, 256 * t:256 * t + 256], T.ls[:, 256 * t:256 * t + 256], "ar%d" % t, ["ls%d" % t])
         if t > 0:
-            for e, a, b in INV_POST:
-                inv_part(e, t, a, b)
-            inv_wrap(t, 1)
-            inv_wrap(t, 2)
-            inv_wrap(t, 3)
+            for e, a0, b0 in INV_POST:
+                inv_part(e, t, a0, b0)
+                if a0 < 8 <= b0:
+                    plain("d0", 0, name, ZI[t], 0)
         else:
-            scatter(7)
-            wrap("pw", 0, T.inv0, quarters("inv0"), "zo", 0, 128)
-            wrap("d0", 0, T.inv0, quarters("inv0"), "zo", 128, 128)
-        if t < RO - 1:
-            name = "inv%d" % (t % 2)
-            dmas("pack", [("Y", T.isn[:, 512 * t:512 * t + 512], T[name][0:128:8, :], quarters(name), ["isn%d" % t])])
-            send(-HOPS[t], T.ir[:, 512 * (t + 1):512 * (t + 2)], T.isn[:, 512 * t:512 * t + 512], "ai%d" % (t + 1), ["isn%d" % t])
-        vcopy(T.li[:, 0:128], T.pw[:, 0:128], ["pw"], ["li0"])
+            for k in range(LATE, 8):
+                scatter(k)
+            plain("d0", 0, name, ZI[t], 0)
+        plain("d1", 0, name, ZI[t], 1)
+        if t == 0:
+            offset_consts(1)
+        if not last:
+            dmas("pack", [("Y", T.isn[:, 1024 * t:1024 * t + 1024], T[name][0:128:4, :], keys(name, 0, 16), ["isn%d" % t])])
+            send(peer(-HOPS[t]), T.ir[:, 1024 * t:1024 * t + 1024], T.isn[:, 1024 * t:1024 * t + 1024], "ai%d" % (t + 1), ["isn%d" % t])
+        if t + 2 < RO:
+            send_x(t + 2)
+        if t == 0:
+            movers(1)
+        if t in (1, 2):
+            inverse_selector(t + 1)
+        copy("V", T.li[:, 0:128], T.d0[:, 0:128], ["d0"], ["li0"])
 
     def conjugate(t):
         last = t == RO - 1
-        h = HOPS[t]
-        c0, c1 = 256 * t, 256 * (t + 1)
-        fk = ["ft%d" % q for q in range(4)]
+        c0 = 256 * t
+        tk, fk = keys("tab", 0, 16), keys("ft", 0, 16)
         for hf in range(2):
             a, m, b = 128 * hf, 128 * hf + F_SHARE[hf], 128 * hf + 128
-            gather("V", T.ft[:, 16 * a:16 * m], T.tab[:, 0:4096], T.li[:, a:m], ["tab", "li%d" % hf], [fk[2 * hf]])
-            gather("S", T.ft[:, 16 * m:16 * b], T.tab[:, 0:4096], T.li[:, m:b], ["tab", "li%d" % hf], [fk[2 * hf + 1]])
+            gather("V", T.ft[:, 16 * a:16 * m], T.tab[:, 0:4096], T.li[:, a:m], tk + ["li%d" % hf], fk[8 * hf:8 * hf + 4])
+            gather("S", T.ft[:, 16 * m:16 * b], T.tab[:, 0:4096], T.li[:, m:b], tk + ["li%d" % hf], fk[8 * hf + 4:8 * hf + 8])
             if hf == 0:
-                vcopy(T.li[:, 128:256], T.d0[:, 0:128], ["d0"], ["li1"])
-        if not last:
-            wrap("pw", 0, T.ft, fk[0:2], "zi", 0, 128)
-        cuts = LAST_CUTS if last else CUTS
+                copy("V", T.li[:, 128:256], T.d1[:, 0:128], ["d1"], ["li1"])
+                if not last:
+                    plain("pk", 256, "ft", ZF, 0)
 
-        def part(q):
-            v = (LAST_SHARE if last else SHARE)[q]
-            for e, a, b, hf in (("V", 64 * q, 64 * q + v, 0), ("S", 64 * q + v, 64 * q + 64, 1)):
-                gather(e, T.fo[:, 16 * a:16 * b], T.ft[:, 0:4096], T.lr[:, c0 + a:c0 + b],
-                       fk + ["lr%d" % t], ["fo%d%s" % (q, "ab"[hf])])
-
-        def fold(q):
-            k = chunk(cuts, q)
-            wrap("d%d" % k, 64 * (q - cuts[k]), T.fo, ["fo%da" % q, "fo%db" % q], "zo", 64 * q, 64)
-
-        def out(k):
-            a, b = 64 * cuts[k], 64 * cuts[k + 1]
-            if last:
-                vcopy(T.ys[:, a:b], T["d%d" % k][:, 0:b - a], ["d%d" % k], ["ys%d" % k])
-                send(sum(HOPS), T.yl[:, a:b], T.ys[:, a:b], "a" + "ab"[k], ["ys%d" % k])
-            else:
-                vcopy(T.lo[:, c1 + a:c1 + b], T["d%d" % k][:, 0:b - a], ["d%d" % k], ["lo%s%d" % ("abc"[k], t + 1)])
+        def part(e, a, b):
+            gather(e, T.fo[:, 256 * a:256 * b], T.ft[:, 0:4096], T.lr[:, c0 + 16 * a:c0 + 16 * b], fk + ["lr%d" % t], keys("fo", a, b))
 
         if last:
-            for q in range(4):
-                part(q)
-                fold(q)
-            out(0)
-            out(1)
-            dmas("st", [("Y", T.yo[:, 0:192], T.yl[:, 0:192], ["yla"], []),
-                        ("S", T.yo[:, 192:256], T.yl[:, 192:256], ["ylb"], [])])
+            for a in range(0, 16, 4):
+                part("V", a, a + 2)
+                part("S", a + 2, a + 4)
+            fold("pl", 0, T.fo, "fo", ZO, LAST, NATURAL[:8], NATURAL[8:], {}, mixed=True)
+            copy("V", T.ys[:], T.pl[:, 0:256], ["pl"], ["ys"])
+            send(peer(sum(HOPS)), T.yl[:], T.ys[:], "ay", ["ys"])
+            dmas("st", [("Y", T.yo[:], T.yl[:], ["yl"], [])])
             return
-        dmas("unp", [("Y", T["inv%d" % (t % 2)][0:128:8, :], T.ir[:, 512 * (t + 1):512 * (t + 2)], ["ir%d" % (t + 1)],
-                      quarters("inv%d" % (t % 2)))])
-        wrap("pw", 128, T.ft, fk[2:4], "zi", 128, 128)
-        for hf in range(2):
-            a, m, b = 128 * hf, 128 * hf + O_SHARE[hf], 128 * hf + 128
-            ka, kb = ["fo%da" % (2 * hf), "fo%db" % (2 * hf)], ["fo%da" % (2 * hf + 1), "fo%db" % (2 * hf + 1)]
-            gather("V", T.fo[:, 16 * a:16 * m], T.ft[:, 0:4096], T.lr[:, c0 + a:c0 + m], fk + ["lr%d" % t], [ka[0], kb[0]])
-            gather("S", T.fo[:, 16 * m:16 * b], T.ft[:, 0:4096], T.lr[:, c0 + m:c0 + b], fk + ["lr%d" % t], [ka[1], kb[1]])
-            wrap("d%d" % hf, 0, T.fo, ka + kb, "zo", a, 128)
-        out(0)
-        window_dmas(T.ow, 512 * (t + 1), "ow%d" % (t + 1), range(8))
-        later["o1"] = lambda: out(1)
-        later["o2"] = lambda: vcopy(T.lf[:, c1:c1 + 256], T.pw[:, 0:256], ["pw"], ["lf%d" % (t + 1)])
+        name = "inv%d" % (t % 2)
+        dmas("unp", [("Y", T[name][0:128:4, :], T.ir[:, 1024 * t:1024 * t + 1024], ["ir%d" % (t + 1)], keys(name, 0, 16))])
+        plain("pk", 384, "ft", ZF, 1)
+        p = 1024 * ((t + 1) % 2)
+        ow = "ow%d" % ((t + 1) % 2)
+        o = order(t)
+        part("V", 8, 12)
+        part("S", 12, 16)
+        fold("pl", 128, T.fo, "fo", ZO, o, o[1:8], o[8:], {"y2": 1})
+        if t == 0:
+            offsets(1, "d0")
+        for a in (0, 4):
+            part("V", a, a + 2)
+            part("S", a + 2, a + 4)
+        if t == 0:
+            copy("S", T.base[:, 64:128], T.d0[:, 0:64], ["d0"], ["base1"])
+        copy("V", T.lx[:, 128:256], T.pl[:, 128:256], ["pl"], ["lx1"])
+        lower_list(t + 1)
+        dmas("owd", [("Y", T.ow[16 * y:16 * y + 16, p:p + 512], T.fo[0:128:8, 512 * y:512 * y + 512],
+                      keys("fo", 2 * y, 2 * y + 2), [ow + "0"]) for y in (4, 5, 6, 7, 0, 1, 2, 3)])
+        dmas("owe", [("Y", T.ow[:, p + 512:p + 1024], T.ow[:, p:p + 512], [ow + "0"], [ow + "1"])])
 
-        def rest():
-            send(-HOPS[t + 1], T.lr[:, c1:c1 + 256], T.lo[:, c1:c1 + 256], "ar%d" % (t + 1), ["loa%d" % (t + 1), "lob%d" % (t + 1)])
-            if t + 2 < RO:
-                send_x(t + 2)
-                round_consts(t + 2)
-        later["rest"] = rest
-
-    def send_x(t):
-        send(-sum(HOPS[:t]), T.xs[:, 4096 * t:4096 * t + 4096], T.xs[:, 0:4096], "ax%d" % t, ["xs0"])
-
-    send_x(1)
-    round_consts(1)
     for t in range(RO):
         scores(t)
         shifts(t)

from concourse.bass import DstId, RemoteDMATransfer
from concourse.mybir import AluOpType, AxisListType, ActivationFunctionType

RO = 6
HOPS = (1, 2, 3, 4, 5, 6)
N = 8
ND = (5, 3, 3, 3, 3, 3)
DUP = 128 * 7
H1 = 2048 + DUP

SCRATCH = {
    "xs": ("sbuf", [128, RO * 4096], "bfloat16"),
    "xo": ("sbuf", [128, H1 + 2048], "bfloat16"),
    "xt": ("sbuf", [128, 2048], "bfloat16"),
    "ml": ("sbuf", [128, 8 * 1024], "bfloat16"),
    "mp": ("sbuf", [128, sum(ND) * 1024], "bfloat16"),
    "tab": ("sbuf", [128, 4096], "bfloat16"),
    "ft": ("sbuf", [128, 4096], "bfloat16"),
    "fo": ("sbuf", [128, 4096], "bfloat16"),
    "inv0": ("sbuf", [128, 4096], "bfloat16"),
    "inv1": ("sbuf", [128, 4096], "bfloat16"),
    "junk": ("sbuf", [128, 1024], "bfloat16"),
    "oi": ("sbuf", [128, 256], "int32"),
    "ln": ("sbuf", [128, 256], "uint16"),
    "lx": ("sbuf", [128, 256], "uint16"),
    "ls": ("sbuf", [128, RO * 256], "uint16"),
    "lr": ("sbuf", [128, RO * 256], "uint16"),
    "lf": ("sbuf", [128, 256], "uint16"),
    "li": ("sbuf", [128, 256], "uint16"),
    "isn": ("sbuf", [128, 5 * 1024], "bfloat16"),
    "ir": ("sbuf", [128, 5 * 1024], "bfloat16"),
    "ow": ("sbuf", [128, 2 * 1024], "bfloat16"),
    "bo": ("sbuf", [128, 1024], "bfloat16"),
    "ys": ("sbuf", [128, 256], "float32"),
    "yl": ("sbuf", [128, 256], "float32"),
    "dm": ("sbuf", [128, 1024], "bfloat16"),
    "pm": ("sbuf", [128, 128], "bfloat16"),
    "idn": ("sbuf", [128, 128], "bfloat16"),
    "zz": ("sbuf", [128, 7 * 144], "bfloat16"),
    "cf": ("sbuf", [128, 576], "float32"),
    "row": ("sbuf", [128, 512], "float32"),
    "one": ("sbuf", [128, 128], "bfloat16"),
    "srow": ("sbuf", [128, 32], "bfloat16"),
    "base": ("sbuf", [128, 128], "float32"),
    "pi": ("sbuf", [128, 8], "int32"),
    "mk": ("sbuf", [128, 4], "float32"),
    "hl": ("sbuf", [128, 512], "bfloat16"),
    "ramp": ("sbuf", [128, 8], "float32"),
    "hc": ("sbuf", [128, 8], "float32"),
    "kl": ("sbuf", [128, 8], "float32"),
    "ks": ("sbuf", [128, RO * 8], "float32"),
    "kr": ("sbuf", [128, RO * 8], "float32"),
    "km": ("sbuf", [128, 4], "float32"),
    "rl": ("sbuf", [128, 64], "uint16"),
    "d0": ("psum", [128, 512], "float32"),
    "d1": ("psum", [128, 512], "float32"),
    "d2": ("psum", [128, 512], "float32"),
    "tb": ("psum", [128, 1024], "bfloat16"),
    "pa": ("psum", [128, 1024], "float32"),
    "pl": ("psum", [128, 512], "float32"),
    "pk": ("psum", [128, 512], "float32"),
}
SEMAPHORES = (["cV", "cS", "cP", "cG", "ldo", "ldx", "tabd", "owd", "owe", "pack", "unp", "sent", "sf", "st", "ay", "fst", "late"]
              + ["%s%d" % (n, t) for n in ("ar", "ax", "ai", "ak") for t in range(RO)]
              + ["af%d_%d" % (t, s) for t in range(RO) for s in range(ND[t])])
PSUM = ("d0", "d1", "d2", "tb", "pa", "pl", "pk")
BIG64 = 1.5 * 2.0 ** 29

Y, J = ["y2", "y1", "y0"], ["j2", "j1", "j0"]
FIELDS = (["b1", "b0"], ["b5", "b2"], ["b4", "b3"])
ROLES = ((0, 2, 1), (0, 2, 1), (1, 0, 2), (2, 0, 1), (2, 0, 1), (1, 0, 2))
NATURAL = Y + ["b5", "b4", "b3", "b2", "b1", "b0"] + J
FIRST = ["y2", "b0"] + J + ["y1", "y0", "b5", "b4", "b3", "b2", "b1"]
STAR = Y + J + ["b0", "b5", "b4", "b3", "b2", "b1"]
LAST = J + ["b1", "b0", "b2"] + Y + ["b5", "b4", "b3"]


def roles(t):
    f, u, v = (FIELDS[k] for k in ROLES[t])
    side = "b%d" % t
    q = [b for b in f if b != side][0]
    if t == 0:
        return side, q, ["b3", "b2"], ["b4", "b5"], u + v
    return side, q, u, v, u + v


def order(t):
    if t == RO - 1:
        return LAST
    side, q, a, c, r = roles(t + 1)
    return Y + J + a + [q, side] + c


def wt(bits):
    return {b: 1 << (len(bits) - 1 - k) for k, b in enumerate(bits)}


def values(bits):
    return [{b: n >> (len(bits) - 1 - k) & 1 for k, b in enumerate(bits)} for n in range(1 << len(bits))]


def dot(w, v):
    return sum(w[b] * v[b] for b in v if b in w)


def pieces(weights):
    dims = []
    for w in weights:
        if dims and w == dims[-1][0] * dims[-1][1]:
            dims[-1][1] *= 2
        else:
            dims.append([w, 2])
    low = dims[:3]
    n = 1
    for d in low:
        n *= d[1]
    nb = n.bit_length() - 1
    out = []
    for h in range(2 ** (len(weights) - nb)):
        off = sum(weights[nb + b] for b in range(len(weights) - nb) if h >> b & 1)
        out.append((h * n, n, off, [list(d) for d in reversed(low)]))
    return out


SEQ = {"V": "g8:9 x0 e0:1 g0:4 u e1:2 g12:14 m3 e2:3 g14:16 m4 e3:4 m5 lf m6 m7 i0:1 kl i1:3",
       "S": "g9:10 g10:12 g4:8 r0 r1 r2 r3 r4 r5 r6 r7 r8 r9 r10 r11 kp r12 r13 r14 r15",
       "G": "f0 f1 f2 K"}
SEQ0 = {"V": "s0 s1 x0 e0:1 g0:3 s2 u e1:2 s3 e2:3 s4 e3:4 m5 m6 m7 s5 kl s6",
        "S": "g8:10 g10:12 c0 g3:8 r0 r1 r2 g12:14 r3 o r4 r5 g14:16 r6 r7 r8 cb r9 r10 r11 r12 kp r13 r14 r15",
        "G": "G0 G1 G2 G3 f0 f1 f2 f3 f4 G4 K G5"}
COST = {"g": 0.39, "u": 0.2, "x": 0.18, "e": 0.27, "r": 0.55, "m": 1.05, "k": 0.1, "i": 0.39, "l": 0.3, "s": 1.85, "c": 0.4,
        "o": 1.1, "f": 0.3, "K": 0.3, "G": 1.3}
START = (4.0, 5.3, 5.1, 6.0)
FOLD, HOP = 1.6, 2.0
LATE = 7
INV_PRE, INV_MID = 3, 5
INV_POST = (("V", 5, 8), ("S", 8, 13), ("V", 13, 16))
F_SHARE = (60, 60)


def rank_program(g, core, T, topo):
    rank = T.rank_of(core)
    if rank is None:
        return
    A = AluOpType
    AF = ActivationFunctionType
    Q = {"V": g.vector, "S": g.scalar, "P": g.tensor, "G": g, "Y": g.sync}
    count = {}
    known = {e: {} for e in Q}
    lastw = {}
    readers = {}

    def wait(e, tok):
        if tok is None or (e == "P" and tok[0] == "cP"):
            return
        if known[e].get(tok[0], 0) < tok[1]:
            Q[e].wait_ge(T.sem[tok[0]], tok[1])
            known[e][tok[0]] = tok[1]

    def deps(e, rd, wr):
        toks = []
        for k in rd:
            toks.append(lastw.get(k))
            if k in PSUM:
                toks += [t for t in readers.get(k, []) if t[0] != "c" + e]
        for k in wr:
            toks.append(lastw.get(k))
            toks += readers.get(k, [])
        best = {}
        for t in toks:
            if t is not None and best.get(t[0], 0) < t[1]:
                best[t[0]] = t[1]
        for s in best:
            wait(e, (s, best[s]))

    def mark(tok, rd, wr):
        for k in rd:
            readers.setdefault(k, []).append(tok)
        for k in wr:
            lastw[k] = tok
            readers[k] = []

    def op(e, fn, rd=(), wr=()):
        deps(e, rd, wr)
        s = "c" + e
        count[s] = count.get(s, 0) + 1
        fn().then_inc(T.sem[s], 1)
        mark((s, count[s]), rd, wr)

    def dmas(sem, items):
        for e, out, in_, rd, wr in items:
            deps(e, rd, wr)
            Q[e].dma_start(out, in_).then_inc(T.sem[sem], 16)
            count[sem] = count.get(sem, 0) + 16
        for e, out, in_, rd, wr in items:
            mark((sem, count[sem]), rd, wr)

    def arrives(key, sem, n):
        count[sem] = n
        lastw[key] = (sem, n)

    def peer(d):
        return T.cores[(rank + d) % N]

    near = [c for c in T.cores if topo.chip(c) == topo.chip(core) and topo.die(c) == topo.die(core)]
    partner = near[near.index(core) ^ 1]

    def width(src, dst):
        return len(topo.engines(src, dst))

    def send(dst, out, in_, sem, rd):
        deps("G", rd, ())
        rid, pid, _ = topo.addr(dst)
        g.remote_dma(out, in_, T.sem[sem], T.sem.sent, pid, rid, topo.mask(core, dst))
        count["sent"] = count.get("sent", 0) + width(core, dst)

    def gather(e, out, win, off, rd, wr):
        if e == "V":
            op(e, lambda: g.vector.tensor_copy(out, win.indirect(off)), rd, wr)
        else:
            op(e, lambda: g.scalar.activation(out, win.indirect(off), AF.Copy), rd, wr)

    def mm(out, lhsT, rhs, start, stop, rd, wr):
        op("P", lambda: g.tensor.matmul(out, lhsT, rhs, start, stop), rd, wr)

    def sel(ap, pat, fill, base, key, cm=1):
        op("G", lambda: g.affine_select(ap, ap, pat, A.not_equal, fill, base, cm), [key], [key])

    def iota(ap, pat, base, cm, key, small=True):
        if small:
            op("G", lambda: g.iota(ap, pat, base, cm, allow_small_or_imprecise_dtypes=True), [], [key])
        else:
            op("G", lambda: g.iota(ap, pat, base, cm), [], [key])

    def memset(ap, v, keys):
        op("V", lambda: g.vector.memset(ap, v), [], keys)

    def copy(e, out, in_, rd, wr):
        if e == "V":
            op(e, lambda: g.vector.tensor_copy(out, in_), rd, wr)
        else:
            op(e, lambda: g.scalar.activation(out, in_, AF.Copy), rd, wr)

    def ts(out, in0, s1, s2, ops, rd, wr):
        op("V", lambda: g.vector.tensor_scalar(out, in0, s1, s2, *ops), rd, wr)

    def keys(name, a, b):
        return ["%s%d" % (name, k) for k in range(a, b)]

    ZO, ZF, Z16, ZW, ZI = 0, 1, 2, 3, (4, 4, 5, 6, 6, 5)

    def zeros(bank, col, n, start):
        mm(T[bank][:, col:col + n], T.zz[0:1, 144:272], T.zz[0:1, 144:144 + n], start, not start, ["zz0", "zz1", "zz2"], [bank])

    def fold(bank, col, src, name, z, so, cols, part, fixed, rows=128, mixed=False, only=None):
        ws, wc, wp = wt(so), wt(cols), wt(part)
        best = []
        for i in range(len(cols)):
            for k in range(i + 1, len(cols) + 1):
                p = so.index(cols[i])
                if so[p:p + k - i] == cols[i:k] and len(best) < k - i <= (6 if only is not None else 8):
                    best = cols[i:k]
        n = 1 << len(best)
        rest = [b for b in cols if b not in best]
        calls = []
        for vc in values(rest):
            for vp in values(part):
                calls.append((dot(ws, vc) + dot(ws, vp) + dot(ws, fixed), dot(wc, vc), dot(wp, vp)))
        if mixed:
            calls.sort()
            zeros(bank, col, 1 << len(cols), True)
        for i, (s0, c0, r) in enumerate(calls):
            if only is not None and i // 16 != only:
                continue
            ss, cs = ws[best[-1]], wc[best[-1]]
            last = s0 + ss * (n - 1)
            a = 144 * z + 15 - r
            mm(T[bank][:, col + c0:col + c0 + cs * (n - 1) + 1:cs], T.zz[0:rows, a:a + 128], src[0:rows, s0:last + 1:ss],
               not mixed and i % 16 == 0, not mixed and i % 16 == 15,
               keys(name, s0 // 256, last // 256 + 1) + ["zz%d" % z], [bank])
        if mixed:
            zeros(bank, col, 1 << len(cols), False)

    def plain(bank, col, name, z, half):
        fold(bank, col, T[name], name, z, NATURAL, NATURAL[1:8], NATURAL[8:], {"y2": half})

    for t in range(RO):
        arrives("lr%d" % t, "ar%d" % t, width(peer(HOPS[t]), core))
        arrives("kr%d" % t, "ak%d" % t, width(partner, core))
        for s in range(ND[t]):
            arrives("mp%d_%d" % (t, s), "af%d_%d" % (t, s), width(partner, core))
        if t > 0:
            arrives("xs%d" % t, "ax%d" % t, width(peer(sum(HOPS[:t])), core))
            arrives("ir%d" % t, "ai%d" % t, width(peer(HOPS[t - 1]), core))
    arrives("yl", "ay", width(peer(-sum(HOPS)), core))

    dmas("ldo", [("Y", T.oi[:], T.o[:], [], ["oi"])])
    dmas("ldx", [("Y", T.xs[:, 0:4096], T.x[:], [], ["xs0"])])
    iota(T.pi[:, 0:4], [[-4, 4]], 16, 1, "pi", False)
    iota(T.ramp[:], [[1, 8]], 0, 0, "ramp")
    memset(T.idn[:], 0.0, ["idn"])
    ts(T.pi[:, 4:8], T.pi[:, 0:4], 15, None, [A.bitwise_and], ["pi"], ["pj"])
    memset(T.dm[:, 512:1024], 0.0, ["dm1"])
    ts(T.mk[:], T.pi[:, 4:8], 0.0, None, [A.is_equal], ["pj"], ["mk"])
    memset(T.pm[:], 0.0, ["pm"])
    ts(T.tab[:, 0:8], T.ramp[:], T.mk[:, 0:1], None, [A.mult], ["ramp", "mk"], ["tab0"])
    ts(T.hc[:], T.ramp[:], T.mk[:, 0:1], 8.0, [A.mult, A.mult], ["ramp", "mk"], ["hc"])
    for k in range(6):
        n = 8 << k
        f = [i for i in range(3) if "b%d" % k in FIELDS[i]][0]
        m = T.mk[:, f + 1:f + 2]
        key = "tab1" if k == 5 else "tab0"
        if FIELDS[f][0] == "b%d" % k:
            ts(T.tab[:, n:2 * n], T.tab[:, 0:n], m, m, [A.add, A.add], ["tab0", "mk"], [key])
        else:
            ts(T.tab[:, n:2 * n], T.tab[:, 0:n], m, None, [A.add], ["tab0", "mk"], [key])
    for k in range(3):
        n = 512 << k
        op("S", lambda: g.scalar.activation(T.tab[:, n:2 * n], T.tab[:, 0:n], AF.Identity, bias=T.hc[:, 1 << k:(1 << k) + 1]),
           keys("tab", 0, n // 256) + ["hc"], keys("tab", n // 256, n // 128))
    memset(T.zz[:, 0:432], 0.0, ["zz0", "zz1", "zz2"])
    ts(T.hl[:, 0:256], T.oi[:], BIG64, -BIG64, [A.add, A.add], ["oi"], ["hl0"])
    memset(T.zz[:, 432:1008], 0.0, ["zz3", "zz4", "zz5", "zz6"])
    op("V", lambda: g.vector.tensor_tensor(T.hl[:, 256:512], T.oi[:], T.hl[:, 0:256], A.subtract), ["oi", "hl0"], ["hl1"])
    dmas("fst", [("Y", T.fo[k:16:2, 2048 * h:2048 * h + 2048], T.hl[:, 256 * k + 128 * h:256 * k + 128 * h + 128],
                  ["hl%d" % k], keys("fo", 8 * h, 8 * h + 8)) for k in range(2) for h in range(2)])
    dmas("late", [("Y", T.inv1[:, 512 * LATE:4096], T.tab[:, 512 * LATE:4096], keys("tab", 2 * LATE, 16), keys("inv1", 2 * LATE, 16))])
    copy("V", T.ln[:], T.oi[:], ["oi"], ["ln"])
    memset(T.cf[:], 0.0, ["z0", "z1", "rm", "pq0", "pq1"])

    sel(T.idn[:], [[-1, 128]], 1.0, 0, "idn")
    for fill, step, base in ((1.0, 0, 0), (-1.0, -16, -1), (-1.0, -16, 127)):
        sel(T.dm[:, 512:1024], [[-16, 8], [-2, 8], [step, 8]], fill, base, "dm1")
    side, q, a, c, r4 = roles(0)
    w = wt(J + a + [q, side])
    for c0, n, off, pat in pieces([-w[b] for b in reversed(NATURAL[5:])]):
        sel(T.pm[:, c0:c0 + n], pat, 1.0, off, "pm")
    for k in range(2):
        sel(T.zz[:, 144 * Z16 + 15:144 * Z16 + 128:16], [[-2, 8]], 1.0, -k, "zz%d" % Z16)

    def selector(z, rows):
        for row, weight in rows:
            sel(T.zz[:, 144 * z + 15:144 * z + 128:16], [[-16, 8]], float(weight), -row, "zz%d" % z)

    def inverse_selector(t):
        selector(ZI[t], [(0, 64)] + [(4 + 4 * f, v) for f, v in zip(ROLES[t], (16, 4, 1))])

    def movers(t):
        side, q, a, c, r4 = roles(t)
        w = wt(FIRST[5:] if t == 0 else a + [q] + Y[1:] + c)
        for v in range(2):
            for c0, n, off, pat in pieces([-w[b] for b in reversed(Y[1:] + r4)]):
                p = 320 + 128 * t + 64 * v + c0
                sel(T.cf[:, p:p + n], pat, -512.0, off - w[q] * v, "pq%d" % t)

    def window_consts():
        sel(T.zz[:, 144 * ZW:144 * ZW + 48], [[-1, 48]], 1.0, 16, "zz%d" % ZW)
        iota(T.one[:], [[0, 128]], 1, 0, "one")

    def key_consts():
        iota(T.srow[:, 0:16], [[0, 2], [64, 8]], 0, 0, "srow")
        iota(T.srow[:, 16:32], [[0, 16]], 0, 0, "srow")
        for h in range(2):
            sel(T.cf[:, 192:320], [[-16, 4], [0, 2], [-1, 16]], 512.0, -64 * h, "rm")

    def list_consts():
        inverse_selector(0)
        selector(ZF, [(4, 1), (12, 1)])
        selector(ZO, [(0, 1), (8, 1)])

    def offset_consts(t):
        side, q, a, c, r4 = roles(t)
        w = wt(STAR[6:] if t == 0 else order(0)[6:])
        if t == 0:
            iota(T.row[:, 384:512], [[0, 128]], 1, 0, "row")
            iota(T.row[:, 0:128], [[0, 8], [w[r4[1]], 4], [0, 4]], 0, 0, "row")
            iota(T.row[:, 128:256], [[0, 32], [w[r4[2]], 2], [w[r4[3]], 2]], 0, 0, "row")
        else:
            iota(T.row[:, 256:384], [[0, 8], [w[r4[1]], 4], [w[r4[3]], 4]], 0, 0, "row")
        for sd in range(2):
            for back in range(2):
                js = [(j - back) % 8 if sd == 0 else (j + 1 - back) % 8 + 8 for j in range(8)]
                j0 = 0
                for j in range(1, 9):
                    if j == 8 or js[j] != js[j - 1] + 1:
                        p = 64 * t + 32 * sd + 16 * back + 2 * j0
                        iota(T.base[:, p:p + 2 * (j - j0)], [[64, j - j0], [w[q], 2]], 64 * js[j0] + w[side] * (1 - sd), 0,
                             "base%d" % t)
                        j0 = j

    def offsets(t, bank):
        out = T[bank][:, 0:64]
        mm(out, T.row[0:1, 384:512], T.base[0:1, 64 * t:64 * t + 64], True, False, ["row", "base%d" % t], [bank])
        for k in ((0, 1), (2,))[t]:
            mm(out, T.row[0:1, 128 * k:128 * k + 128], T.row[0:1, 384:448], False, k > 0, ["row"], [bank])

    def first_window(part):
        ws, ww = wt(FIRST), wt(STAR[3:])
        for v in values(["b0"] + J)[2 * part:2 * part + 2]:
            for y in values(Y):
                p, s0, c0 = 32 * (2 * y["y2"] + y["y1"]), dot(ws, v) + dot(ws, y), dot(ww, v)
                z = 144 * ZW + 16 - 16 * y["y0"]
                mm(T.pa[p:p + 32, c0:c0 + 32], T.zz[0:16, z:z + 32], T.fo[0:16, s0:s0 + 32], y["y0"] == 0, y["y0"] == 1,
                   keys("fo", 0, 16) + ["zz%d" % ZW], ["pa"])

    def send_x(t):
        send(peer(-sum(HOPS[:t])), T.xs[:, 4096 * t:4096 * t + 4096], T.xs[:, 0:4096], "ax%d" % t, ["xs0"])

    consts = [lambda: send_x(1), window_consts, key_consts, lambda: movers(0), lambda: offset_consts(0), list_consts]

    def inv_part(e, t, a, b):
        old, new = "inv%d" % ((t - 1) % 2), "inv%d" % (t % 2)
        gather(e, T[new][:, 256 * a:256 * b], T[old][:, 0:4096], T.lf[:, 16 * a:16 * b], keys(old, 0, 16) + ["lf"], keys(new, a, b))

    def scatter(q):
        src = "inv1" if q >= LATE else "tab"
        op("V", lambda: g.vector.tensor_copy(T.inv0[:, 0:4096].indirect(T.ln[:, 32 * q:32 * q + 32]), T[src][:, 512 * q:512 * q + 512]),
           keys(src, 2 * q, 2 * q + 2) + ["ln"], keys("inv0", 0, 16))

    def lower_list(t):
        side, q, a, c, r4 = roles(t)
        if t == 0:
            fold("d2", 0, T.fo, "fo", Z16, FIRST, FIRST[1:8], FIRST[8:], {"y2": 0}, rows=16)
        else:
            fold("d2", 0, T.fo, "fo", ZO, order(t - 1), [side] + J + a + [q], Y[1:] + c, {"y2": 0}, mixed=True)

    def scores(t):
        side, q, a, c, r4 = roles(t)
        w4 = wt(r4)
        nd, m0 = ND[t], sum(ND[:t])
        dk = min(t, 1)
        zc = 96 * dk
        pad = w4[a[0]] + w4[a[1]]
        seq = {e: v.split() for e, v in (SEQ0 if t == 0 else SEQ).items()}
        every = seq["V"] + seq["S"]

        def span(s):
            return [int(v) for v in s[1:].split(":")]

        def covering(kind, k):
            return [s for s in every if s[0] == kind and span(s)[0] <= k < span(s)[1]]

        def gathered(a0, b0):
            return [s for k in range(a0, b0) for s in covering("g", k)]

        def sums(col, src, p, key):
            for j in range(8):
                mm(T.pl[:, col:col + 1], src[:, p + 128 * j:p + 128 * j + 128], T.one[:, 0:1], j == 0, j == 7, [key, "one"], ["pl"])

        def move(src, a0, b0, key, v):
            for k in (v, 2 + v):
                p = 320 + 128 * dk + 64 * v
                mm(T.pk[0:64, 8 * k + a0:8 * k + b0], T.cf[:, p:p + 64], src, False, False, [key, "pq%d" % dk], ["pk"])

        def turn(k):
            for b in range(4):
                p = H1 + 512 * k
                in_ = T.xo[:, p + 128 * b:p + 128 * b + 128] if t == 0 else T.xo[:, p + b:p + 512:4]
                o = 512 * (k % 2) + 128 * b
                op("P", lambda: g.tensor.transpose(T.tb[:, o:o + 128], in_, T.idn[:]), keys("xo", 8 + 2 * k, 10 + 2 * k) + ["idn"], ["tb"])

        def differences(k):
            bank = "d%d" % (k % 3)
            for m in range(4):
                p = 512 * dk + 128 * m
                mm(T[bank][:, 128 * m:128 * m + 128], T.dm[:, p:p + 128], T.xt[:, 128 * k:128 * k + 128], True, True,
                   ["dm%d" % dk, "xt%d" % (k // 4)], [bank])

        def side_zero(h):
            mm(T.pa[:, 512 * h:512 * h + 512], T.idn[:], T.xo[:, 512 * h:512 * h + 512], True, True,
               keys("xo", 2 * h, 2 * h + 2) + ["idn"], ["pa"])

        def upper_keys(h):
            if h == 0:
                mm(T.pk[:, 0:32], T.one[0:1, 0:128], T.srow[0:1, 0:32], True, False, ["one", "srow"], ["pk"])
            for k in range(4):
                p = zc + 48 * h + pad - w4[a[0]] * (k // 2) - w4[a[1]] * (k % 2)
                mm(T.pk[64 + 32 * h:96 + 32 * h, 0:32], T.cf[:, p:p + 32], T.cf[:, 192 + 32 * k:224 + 32 * k], False,
                   False, ["rm"] + keys("sc", 8 * h, 8 * h + 8), ["pk"])
            if h == 1:
                zeros("pk", 0, 32, False)

        def out_list(k):
            o = order(t)
            if t == 0:
                fold("pl", 256, T.fo, "fo", Z16, STAR, o[:8], o[8:], {}, rows=16, only=k)
            else:
                fold("pl", 256, T.fo, "fo", ZO, order(t - 1), o[:8], o[8:], {}, only=k)

        pe = {}
        if t == 0:
            pe["x"] = (0.95, [], lambda: lower_list(0))
            pe["C0"] = (0.25, [], lambda: mm(T.pk[:, 0:512], T.pm[:], T.dm[:, 512:1024], True, True, ["pm", "dm1"], ["pk"]))
        else:
            pe["x"] = (0.5, [], lambda: None)
        for k in range(16):
            pe["d%d" % k] = (0.24, covering("e", k // 4) + (["r%d" % (k - 3)] if k > 2 else ["x0"]) + (["c0"] if t == 0 else []),
                             lambda k=k: differences(k))
        for k in range(4):
            pe["t%d" % k] = (0.24, gathered(8 + 2 * k, 10 + 2 * k) + (covering("e", k - 2) if k > 1 else []), lambda k=k: turn(k))
        for k in range(8 if t == 0 else 0):
            pe["W%d" % k] = (0.25, ["G1", "x0"], lambda k=k: first_window(k))
        for h in range(2):
            pe["a%d" % h] = (0.24, gathered(2 * h, 2 * h + 2) + (["o"] if t == 0 else []), lambda h=h: side_zero(h))
        for k in range(nd):
            pe["p%d" % k] = (0.25, ["A%d" % k], lambda k=k: sums(8 + k, T.mp, 1024 * (m0 + k), "mp%d_%d" % (t, k)))
        for k in range(nd, 8):
            pe["n%d" % k] = (0.25, ["m%d" % k], lambda k=k: sums(k, T.ml, 1024 * k, "ml%d" % k))
        if t == 0:
            pe["CB"] = (0.3, ["G4", "c0"], lambda: offsets(0, "pk"))
        for k in range(4):
            pe["w%d" % k] = (0.5, ["O"] if t == 0 else ["a0", "a1", "d%d" % (3 + 2 * k)], lambda k=k: out_list(k))
        pe["k0"] = (0.3, ["r7"] + (["G2", "cb"] if t == 0 else ["lf"]), lambda: upper_keys(0))
        for v in range(2):
            pe["kL%d" % v] = (0.25, ["kl", "k0"], lambda v=v: move(T.kl[:, nd:8], nd, 8, "kl", v))
            pe["kR%d" % v] = (0.25, ["R", "k0"], lambda v=v: move(T.kr[:, 8 * t:8 * t + nd], 0, nd, "kr%d" % t, v))
        pe["k1"] = (0.25, ["r15", "kL0", "kL1", "kR0", "kR1"], lambda: upper_keys(1))

        def needs(s):
            if s[0] == "g":
                return ["x0"] if span(s)[0] < 8 else []
            if s[0] == "e":
                return ["t%d" % k for k in range(*span(s))]
            if s[0] == "f":
                return gathered(0, 8) + (["u"] if s != "f0" else [])
            if s[0] in "rm":
                return ["d" + s[1:]] if s[0] == "r" else ["a0", "a1"] + gathered(4, 8)
            return {"u": gathered(4, 8), "x0": ["x"], "c0": ["C0"], "cb": ["CB"], "o": ["W%d" % k for k in range(8)], "K": ["kp"],
                    "kp": ["p%d" % k for k in range(nd)], "kl": ["n%d" % k for k in range(nd, 8)]}.get(s, ["lf"] if s[0] == "i" else [])

        def call(e, s):
            n = span(s) if s[1:2].isdigit() else []
            if s[0] == "g":
                p = 256 * n[0] + (DUP if n[0] >= 8 else 0)
                lst, key = (T.ln, "ln") if t == 0 and n[0] >= 8 else (T.lx, "lx%d" % (n[0] // 8))
                gather(e, T.xo[:, p:p + 256 * (n[1] - n[0])], T.xs[:, 4096 * t:4096 * t + 4096], lst[:, 16 * n[0]:16 * n[1]],
                       ["xs%d" % t, key], keys("xo", n[0], n[1]))
            elif s == "u":
                copy(e, T.xo[:, 2048:2048 + 128 * (nd - 1)], T.xo[:, 1024:1024 + 128 * (nd - 1)], keys("xo", 4, 8), ["dup"])
            elif s[0] == "f":
                rd = keys("xo", 0, 8) + (["dup"] if n[0] else [])
                deps("G", rd, ())
                rid, pid, _ = topo.addr(partner)
                p, b = 1024 * (m0 + n[0]), 1024 + 128 * n[0]
                g.remote_dma_fused([RemoteDMATransfer(
                    dst_ids=[DstId(rid=rid, pnc=pid)], dma_engine_mask=topo.mask(core, partner),
                    remote_sem=T.sem["af%d_%d" % (t, n[0])], srcs=[T.xo[:, 0:1024], T.xo[:, b:b + 1024]],
                    dsts=[T.mp[:, p:p + 1024]], alu_op=3)], local_sem=T.sem.sf)
                count["sf"] = count.get("sf", 0) + width(core, partner)
                for k in rd:
                    readers[k] = [tok for tok in readers.get(k, []) if tok[0] != "sf"] + [("sf", count["sf"])]
            elif s == "x0":
                copy(e, T.lx[:, 0:128], T.d2[:, 0:128], ["d2"], ["lx0"])
            elif s[0] == "e":
                o = 512 * (n[0] % 2)
                copy(e, T.xt[:, 512 * n[0]:512 * n[1]], T.tb[:, o:o + 512 * (n[1] - n[0])], ["tb"], keys("xt", n[0], n[1]))
            elif s[0] == "r":
                k = n[0]
                hi, lo = (c[1], c[0]) if t == 0 else c
                col = zc + 48 * (k // 8) + pad + 16 * (k // 4 % 2) + w4[hi] * (k // 2 % 2) + w4[lo] * (k % 2)
                j, bank = 512 * (k % 2), "d%d" % (k % 3)
                op(e, lambda: g.scalar.activation(T.junk[:, j:j + 512], T[bank][:, 0:512], AF.Abs, accum_out=T.cf[:, col:col + 1]),
                   [bank, "z%d" % dk], ["sc%d" % k, "junk%d" % (k % 2)])
            elif s[0] == "m":
                k = n[0]
                deps(e, (), ["ml%d" % k])
                for a0, b0, w in ((0, k, 8 - k), (8 - k, 0, k)):
                    p = 1024 * k + 128 * a0
                    op(e, lambda: g.vector.tensor_tensor(T.ml[:, p:p + 128 * w], T.xo[:, 1024 + 128 * b0:1024 + 128 * (b0 + w)],
                                                         T.pa[:, 128 * a0:128 * (a0 + w)], A.min),
                       keys("xo", 4, 8) + ["pa"], ["ml%d" % k] if a0 else [])
            elif s == "kp":
                copy(e, T.ks[:, 8 * t:8 * t + nd], T.pl[:, 8:8 + nd], ["pl"], ["ks%d" % t])
            elif s == "K":
                send(partner, T.kr[:, 8 * t:8 * t + nd], T.ks[:, 8 * t:8 * t + nd], "ak%d" % t, ["ks%d" % t])
            elif s == "kl":
                copy(e, T.kl[:, nd:8], T.pl[:, nd:8], ["pl"], ["kl"])
            elif s[0] == "i":
                inv_part(e, t, n[0], n[1])
            elif s == "lf":
                copy(e, T.lf[:], T.pk[:, 256:512], ["pk"], ["lf"])
            elif s == "o":
                for h in range(2):
                    copy(e, T.ow[:, 512 * h:512 * h + 512], T.pa[:, 0:512], ["pa"], ["ow0%d" % h])
                dmas("owd", [("Y", T.fo[0:16, 512 * y:512 * y + 512], T.ow[16 * y:16 * y + 16, 0:512], ["ow00"],
                              keys("fo", 0, 16)) for y in range(8)])
            elif s[0] == "s":
                scatter(n[0])
            elif s == "c0":
                copy(e, T.dm[:, 0:512], T.pk[:, 0:512], ["pk"], ["dm0"])
            elif s == "cb":
                copy(e, T.base[:, 0:64], T.pk[:, 0:64], ["pk"], ["base0"])
            else:
                consts[n[0]]()

        lands = {"K": "R", "o": "O"}
        done, steps = {}, []
        clock = dict(zip("VSGP", START if t == 0 else (0.0,) * 4))
        left = list(pe)
        while left or any(seq[e] for e in "VSG"):
            cand = []
            for e in "VSGP":
                for s in (left if e == "P" else seq[e][:1]):
                    need = pe[s][1] if e == "P" else needs(s)
                    if all(k in done for k in need):
                        cand.append((max([clock[e]] + [done[k] + 0.1 for k in need]), len(cand), e, s))
            at, _, e, s = min(cand)
            if e == "P":
                left.remove(s)
                clock[e] = at + pe[s][0]
            else:
                seq[e].pop(0)
                clock[e] = at + COST[s[0]] * (span(s)[1] - span(s)[0] if ":" in s else 1)
            done[s] = clock[e]
            if s[0] == "f":
                done["A" + s[1:]] = max(clock[e] + 1.0, done.get("A%d" % (int(s[1:]) - 1), 0.0)) + FOLD
            if s in lands:
                done[lands[s]] = clock[e] + HOP
            steps.append((e, s))
        for e, s in steps:
            if e == "P":
                pe[s][2]()
            else:
                call(e, s)

    def shifts(t):
        side, q, a, c, r4 = roles(t)
        last = t == RO - 1
        name = "inv%d" % (t % 2)
        dk = min(t, 1)
        if t > 0:
            inv_part("S", t, INV_PRE, INV_MID)
        for k in range(4):
            op("V", lambda: g.vector.tensor_reduce(T.km[:, k:k + 1], T.pk[:, 8 * k:8 * k + 8], AxisListType.X, A.min),
               ["pk"], ["km%d" % k])
        n = 1 if last else 2
        w = wt(FIELDS[ROLES[t][0]])
        for sd in range(2):
            for v in range(2):
                p, o = 64 * dk + 32 * sd + v, w[side] * sd + w[q] * v
                ts(T.rl[:, o:32 * n:4], T.base[:, p:p + 16 * n - 1:2], T.km[:, v:v + 1], T.km[:, 2 + v:3 + v],
                   [A.subtract, A.add] if sd else [A.add, A.subtract], ["base%d" % dk, "km%d" % v, "km%d" % (2 + v)], ["rl%d" % o])
        p = 1024 * (t % 2)
        win = T.ow[:, p:p + 1024]
        rd = keys("rl", 0, 4) + ["ow%d0" % (t % 2), "ow%d1" % (t % 2)]
        gather("V", T.bo[:, 0:256 * n], win, T.rl[:, 0:16 * n], rd, ["boa"])
        gather("S", T.bo[:, 256 * n:512 * n], win, T.rl[:, 16 * n:32 * n], rd, ["bob"])
        dmas("tabd", [("YS"[y % 2], T.tab[0:128:8 // n, 512 * y:512 * y + 512], T.bo[16 * y:16 * y + 16, 0:512 * n],
                       ["boa", "bob"], keys("tab", 2 * y, 2 * y + 2)) for y in range(8)])
        copy("V", T.ls[:, 256 * t:256 * t + 256], T.pl[:, 256:512], ["pl"], ["ls%d" % t])
        send(peer(-HOPS[t]), T.lr[:, 256 * t:256 * t + 256], T.ls[:, 256 * t:256 * t + 256], "ar%d" % t, ["ls%d" % t])
        if t > 0:
            for e, a0, b0 in INV_POST:
                inv_part(e, t, a0, b0)
                if a0 < 8 <= b0:
                    plain("d0", 0, name, ZI[t], 0)
        else:
            for k in range(LATE, 8):
                scatter(k)
            plain("d0", 0, name, ZI[t], 0)
        plain("d1", 0, name, ZI[t], 1)
        if t == 0:
            offset_consts(1)
        if not last:
            dmas("pack", [("Y", T.isn[:, 1024 * t:1024 * t + 1024], T[name][0:128:4, :], keys(name, 0, 16), ["isn%d" % t])])
            send(peer(-HOPS[t]), T.ir[:, 1024 * t:1024 * t + 1024], T.isn[:, 1024 * t:1024 * t + 1024], "ai%d" % (t + 1), ["isn%d" % t])
        if t + 2 < RO:
            send_x(t + 2)
        if t == 0:
            movers(1)
        if t in (1, 2):
            inverse_selector(t + 1)
        copy("V", T.li[:, 0:128], T.d0[:, 0:128], ["d0"], ["li0"])

    def conjugate(t):
        last = t == RO - 1
        c0 = 256 * t
        tk, fk = keys("tab", 0, 16), keys("ft", 0, 16)
        for hf in range(2):
            a, m, b = 128 * hf, 128 * hf + F_SHARE[hf], 128 * hf + 128
            gather("V", T.ft[:, 16 * a:16 * m], T.tab[:, 0:4096], T.li[:, a:m], tk + ["li%d" % hf], fk[8 * hf:8 * hf + 4])
            gather("S", T.ft[:, 16 * m:16 * b], T.tab[:, 0:4096], T.li[:, m:b], tk + ["li%d" % hf], fk[8 * hf + 4:8 * hf + 8])
            if hf == 0:
                copy("V", T.li[:, 128:256], T.d1[:, 0:128], ["d1"], ["li1"])
                if not last:
                    plain("pk", 256, "ft", ZF, 0)

        def part(e, a, b):
            gather(e, T.fo[:, 256 * a:256 * b], T.ft[:, 0:4096], T.lr[:, c0 + 16 * a:c0 + 16 * b], fk + ["lr%d" % t], keys("fo", a, b))

        if last:
            for a in range(0, 16, 4):
                part("V", a, a + 2)
                part("S", a + 2, a + 4)
            fold("pl", 0, T.fo, "fo", ZO, LAST, NATURAL[:8], NATURAL[8:], {}, mixed=True)
            copy("V", T.ys[:], T.pl[:, 0:256], ["pl"], ["ys"])
            send(peer(sum(HOPS)), T.yl[:], T.ys[:], "ay", ["ys"])
            dmas("st", [("Y", T.yo[:], T.yl[:], ["yl"], [])])
            return
        name = "inv%d" % (t % 2)
        dmas("unp", [("Y", T[name][0:128:4, :], T.ir[:, 1024 * t:1024 * t + 1024], ["ir%d" % (t + 1)], keys(name, 0, 16))])
        plain("pk", 384, "ft", ZF, 1)
        p = 1024 * ((t + 1) % 2)
        ow = "ow%d" % ((t + 1) % 2)
        o = order(t)
        part("V", 8, 12)
        part("S", 12, 16)
        fold("pl", 128, T.fo, "fo", ZO, o, o[1:8], o[8:], {"y2": 1})
        if t == 0:
            offsets(1, "d0")
        for a in (0, 4):
            part("V", a, a + 2)
            part("S", a + 2, a + 4)
        if t == 0:
            copy("S", T.base[:, 64:128], T.d0[:, 0:64], ["d0"], ["base1"])
        copy("V", T.lx[:, 128:256], T.pl[:, 128:256], ["pl"], ["lx1"])
        lower_list(t + 1)
        dmas("owd", [("Y", T.ow[16 * y:16 * y + 16, p:p + 512], T.fo[0:128:8, 512 * y:512 * y + 512],
                      keys("fo", 2 * y, 2 * y + 2), [ow + "0"]) for y in (4, 5, 6, 7, 0, 1, 2, 3)])
        dmas("owe", [("Y", T.ow[:, p + 512:p + 1024], T.ow[:, p:p + 512], [ow + "0"], [ow + "1"])])

    for t in range(RO):
        scores(t)
        shifts(t)
        conjugate(t)
    for s in count:
        wait("G", (s, count[s]))
